import numpy as np, ml_dtypes
CORES = [16,18,20,22]
N = 4
import mx_ref
BF = ml_dtypes.bfloat16
def gentries(a):
    return np.ascontiguousarray(a.reshape(8, 16, -1).transpose(0, 2, 1)).reshape(8, -1)
def gtable(e):
    e = np.asarray(e); return np.ascontiguousarray(e.reshape(8, -1, 16).transpose(0, 2, 1)).reshape(128, -1).astype(np.int32)
def gcols(t, e):
    v = np.concatenate([t.reshape(8, 16, -1, 4), np.zeros((8, 16, 1, 4), BF)], axis=2)
    return np.ascontiguousarray(np.stack([v[g][:, e[g]] for g in range(8)])).reshape(128, -1)
def tile(rs):
    return np.stack(rs, axis=2).reshape(128, -1).astype(BF)
def pick(q, e):
    c = np.concatenate([q[0].reshape(128, -1, 4), np.zeros((128, 1, 4), np.uint8)], axis=1); s = np.concatenate([q[1], np.ones((16, 1), np.uint8)], axis=1)
    return (np.ascontiguousarray(c[:, e].reshape(128, -1)), np.ascontiguousarray(s[:, e]))
def join(*qs):
    return (np.concatenate([q[0] for q in qs], axis=1), np.concatenate([q[1] for q in qs], axis=1))
def put(q, e, v):
    c, s = q[0].reshape(128, -1, 4).copy(), q[1].copy(); c[:, e] = v[0].reshape(128, -1, 4); s[:, e] = v[1]
    return (c.reshape(128, -1), s)
def pk(c, s):
    return (np.ascontiguousarray(c), mx_ref.live(s))
def emit(q):
    return q[0], q[1]
def packed(v, rng):
    q = [mx_ref.quantize(np.ascontiguousarray(v[r])) for r in range(N)]
    return np.stack([a for a, b in q]), np.stack([mx_ref.plane(b, rng) for a, b in q])
def values_of_codes():
    e, c = np.zeros((128, 128, 4), np.float32), np.zeros((128, 2, 4), np.uint8)
    e[np.arange(128), np.arange(128), 0] = 1
    c[:127, :, 0] = np.arange(256).reshape(2, 128).T[:127]
    return mx_ref.matmul(mx_ref.quantize(e.reshape(128, 512).astype(BF)), (c.reshape(128, 8), np.full((16, 2), 127, np.uint8))).T.reshape(-1).astype(np.float64)
CODE_VALUE, SCALE_VALUE = values_of_codes(), 2.0 ** (np.arange(256) - 127.0)
def decode(q):
    return (CODE_VALUE[q[0]].reshape(16, 8, -1, 4) * SCALE_VALUE[q[1]][:, None, :, None] + 0.0).reshape(128, -1).astype(np.float32)
def f(rng, *shape):
    return mx_ref.flush((rng.standard_normal(shape, dtype=np.float32) * np.exp2(rng.integers(-2, 3, shape[:-1] + (1,)))).astype(BF))
def wide(rng, *shape, cols=0):
    v = rng.standard_normal(shape, dtype=np.float32) * np.exp2(rng.integers(-12, 13, shape)).astype(np.float32)
    if cols: v *= np.repeat(np.exp2(rng.integers(-cols, cols + 1, shape[:-2] + (1, shape[-1] // 4))) * (rng.random(shape[:-2] + (1, shape[-1] // 4)) > 0.0625), 4, axis=-1).astype(np.float32)
    return mx_ref.flush(v.astype(BF))
C, G, E, K, S = 384, 12, 6, 64, 256
STRIDE = [4, 2, 1]
DIR = [(-1, 0), (-1, 1), (0, 1), (1, 1), (1, 0), (1, -1), (0, -1), (-1, -1)]
def around(e, h):
    return np.stack([np.roll(e[:, g].reshape(N * G, 32), (-h * DIR[g][0], -h * DIR[g][1]), axis=(0, 1)).reshape(N, C) for g in range(8)], axis=1)
def numbers_of(rng):
    return {"x": np.array(f(rng, N, 128, 4 * C)), "u": np.array(f(rng, N, 128, 512)), "v": np.array(f(rng, N, 128, 512))}
def pointers(rng):
    return np.stack([gtable(rng.integers(0, S, (8, C))) for r in range(N)])
def same(rng, w):
    c, s = packed(np.stack([w] * N), rng)
    return {"wc": c, "ws": np.stack([s[0]] * N)}
def weights(rng, still=[]):
    w = np.array(f(rng, 128, 2048)).reshape(8, 16, 4, 8, 16, 4)
    for i in still:
        w[:, i] = 0
        w[:, :, :, :, i] = 0
    return same(rng, w.reshape(128, 2048))
def setup_inputs(rng):
    return {**numbers_of(rng), "p": pointers(rng), **weights(rng)}
def setup_inputs_ties(rng):
    d = numbers_of(rng)
    x = d["x"].reshape(N, 8, 16, C, 4)
    k = np.where(rng.random((N, 1, C)) < 0.5, 4, rng.integers(0, 3, (N, 1, C))) * np.ones((1, 8, 1))
    k[:, :, ::E] = rng.integers(0, 3, (N, 8, K))
    x[:, :, 0] = 0
    x[:, :, 0, :, 0] = k.astype(np.float32).astype(BF)
    u = d["u"].reshape(N, 128, 128, 4)
    u[:, :, ::16] = 0
    o = rng.permutation(N)
    for r in range(N):
        for h in range(0, 128, 16): u[r, h, h, 0] = 0.0 if r == o[0] else -1.0 if r == o[1] else 1.0
    return {"x": x.reshape(N, 128, 4 * C), "u": u.reshape(N, 128, 512), "v": d["v"], "p": pointers(rng), **weights(rng, [0])}
def setup_inputs_near(rng):
    d = numbers_of(rng)
    x = d["x"].astype(np.float32).reshape(N, 8, 16, C, 4)
    x[:, :, 0] = 0
    x[:, :, 8:] = 0
    x[:, :, 0, :, 0] = rng.integers(0, 2, (N, 1, C)) * 2.0 - 1.0
    x[:, :, 0, ::E] = 0
    s = rng.integers(0, 16, (N, 8, K))
    x[:, :, 8, ::E] = ((s[:, :, :, None] >> np.arange(4)) & 1) * np.exp2(np.arange(4) - 23.0)
    x[:, :, 10, :, 0] = (np.where(np.arange(8) < 4, -1.0, -1.125) * 2.0 ** -30)[:, None]
    x[:, :, 10, ::E, 0] = rng.integers(0, 2, (N, 8, K)) * 2.0 ** -30
    u = d["u"].reshape(N, 128, 128, 4)
    u[:, :, ::16] = 0
    o = rng.permutation(N) % 4
    for r in range(N):
        k = 1.0 if o[r] == 0 else 2.0 ** -30
        far = rng.permutation(8)
        if o[r] < 2:
            x[r, :, 11, :, 0] = -2.0 ** -10
            x[r, :, 11, ::E, 0] = 0
        for h in range(0, 128, 16):
            if o[r] < 2:
                u[r, h, h, 0] = k
                u[r, h + 11, h, 0] = k
            if o[r] == 2 and 16 * far[0] == h: u[r, h, h, 0] = 1.0
            if o[r] == 2 and 16 * far[1] == h: u[r, h, h, 0] = -1.0
            if o[r] < 3: u[r, h + 8, h] = k
            else: u[r, h + 10, h, 0] = k * 1.125 if h >= 64 else k * 1.25
    return {"x": x.reshape(N, 128, 4 * C).astype(BF), "u": u.reshape(N, 128, 512), "v": d["v"], "p": pointers(rng), **weights(rng, [0, 8, 9, 10, 11, 12, 13, 14, 15])}
def setup_inputs_huge(rng):
    d = numbers_of(rng)
    o = rng.permutation(N)
    c = rng.integers(0, 2, (N, 1, 1, C, 1)) * 2.0 - 1.0
    x = (0.6 + 0.09 * rng.random((N, 8, 16, C, 4))) * 2.0 ** 30 * c
    x[o == 0] = 0.875 * 2.0 ** 30 * c[o == 0]
    x[:, :, :, ::E] = (rng.random((N, 8, 1, K, 1)) * 2.0 - 1.0) * (0.8 + 0.2 * rng.random((N, 8, 16, K, 4))) * 2.0 ** 26
    a = 2.0 ** 29 * (1.0 - 0.1 * rng.random((N, 8, 16, 8, 4)))
    for g in range(8): a[:, g, :, g] *= 2.0
    for r in range(N):
        if o[r] == 0:
            a[r] = 2.0 ** 30
            for g in range(8): a[r, 0, :7 - g, g] *= 0.5
        if o[r] < N // 2: a[r] *= (rng.permutation(8) % 2 * 2.0 - 1.0)[None, None, :, None]
    u = d["u"].reshape(N, 128, 128, 4)
    u[:, :, ::16] = a.reshape(N, 128, 8, 4).astype(np.float32).astype(BF)
    w = np.zeros((128, 4, 128, 4), np.float32)
    i = np.arange(128)
    for b in range(4): w[i, b, i, b] = 4
    return {"x": x.astype(np.float32).reshape(N, 128, 4 * C).astype(BF), "u": u.reshape(N, 128, 512), "v": d["v"], "p": pointers(rng), **same(rng, w.reshape(128, 2048).astype(BF))}
def setup_inputs_few(rng):
    d = numbers_of(rng)
    e = rng.permutation(N)
    t = K * e[0] + rng.integers(0, K, (N, 8, C))
    t[e[0]] = S - 1
    t[e[1]] = 0
    t[e[2]] = K * e[2] + rng.integers(0, K, (8, C))
    t[e[3]] = rng.integers(0, S, (8, 1))
    return {**d, "p": np.stack([gtable(t[r]) for r in range(N)]), **weights(rng)}
def setup_inputs_spread(rng):
    d = setup_inputs(rng)
    d["x"] = wide(rng, N, 128, 4 * C, cols=6)
    return d
def check_inputs(d):
    b = []
    for k in ("x", "u", "v"):
        a = np.abs(d[k].astype(np.float32))
        if not (np.isfinite(a).all() and ((a == 0) | (a >= 2.0 ** -30) & (a <= 2.0 ** 30)).all()): b.append("a value of " + k)
    if not ((d["p"] >= 0) & (d["p"] < S)).all(): b.append("an entry of p")
    if ((d["wc"] & 0x7F) == 0x7F).any(): b.append("a code of wc that is no number")
    for k in ("wc", "ws"):
        if (d[k] != d[k][:1]).any(): b.append(k + " isn't the same on all ranks")
    z = np.zeros((128, 4, 4), np.float32)
    z[:, 1] = 2.0 ** -30
    z[:, 2] = 2.0 ** 30
    c, s = emit(mx_ref.quantize(z.reshape(128, 16).astype(BF)))
    for r in range(N):
        a = mx_ref.live(d["ws"][r])
        if not ((a == s[0, 0]) | (a >= s[0, 1]) & (a <= s[0, 2])).all(): b.append("a scale of ws")
    return b
def reference(x, u, v, p, wc, ws):
    qu = [mx_ref.quantize(u[r]) for r in range(N)]
    lay = [pk(wc[r], ws[r]) for r in range(N)]
    now = [x[r] for r in range(N)]
    ptr = np.stack([gentries(p[r]) for r in range(N)])
    for h in STRIDE:
        own = [decode(mx_ref.quantize(now[r])) for r in range(N)]
        seeds = np.concatenate([own[r].reshape(128, C, 4)[:, ::E] for r in range(N)], axis=1).reshape(128, 4 * S).astype(BF)
        came, new = around(ptr, h), []
        for r in range(N):
            z = (gcols(seeds, came[r]).astype(np.float32) - own[r]).astype(BF)
            s = mx_ref.matmul(qu[r], mx_ref.quantize(z))[::16] + np.float32(0.0)
            new.append(np.take_along_axis(came[r], np.argsort(-s, axis=0, kind="stable"), axis=0))
        ptr = np.stack(new)
        again = around(ptr, h)
        for r in range(N):
            q = mx_ref.quantize(gcols(seeds, again[r]))
            now[r] = tile([np.maximum(mx_ref.matmul(pick(lay[r], np.arange(128 * b, 128 * b + 128)), q), np.float32(0.0)) * np.float32(0.015625) + own[r][:, b::4] for b in range(4)])
    y, op = np.zeros((N, 128, C), np.float32), np.zeros((N, 8, C), np.float32)
    oc, osc = np.zeros((N, 128, 4 * C), np.uint8), np.zeros((N, 16, C), np.uint8)
    for r in range(N):
        q = mx_ref.quantize(now[r])
        y[r] = mx_ref.matmul(mx_ref.quantize(v[r]), q)
        op[r] = ptr[r]
        oc[r], osc[r] = emit(q)
    return {"y": y, "op": op, "oc": oc, "osc": osc}

@@ -1,0 +1,598 @@
+from concourse.bass import DstId, RemoteDMATransfer
+from concourse.mybir import dt, AluOpType, ActivationFunctionType
+
+C = 384
+H = [4, 2, 1]
+DC = [0, 1, 1, 1, 0, -1, -1, -1]
+
+SCRATCH = {}
+
+
+def _b(name, cols, dtype, where="sbuf"):
+    SCRATCH[name] = (where, [128, cols], dtype)
+
+
+X4, U8, BF, F32, I32, U16 = "float8_e4m3fn_x4", "uint8", "bfloat16", "float32", "int32", "uint16"
+for _i in range(8):
+    _b("ps%d" % _i, 512, F32, "psum")
+for _r in range(4):
+    _b("xt%d" % _r, 4 * C, BF)
+    _b("qx%d" % _r, C, X4)
+    _b("sx%d" % _r, C, U8)
+    _b("ext%d" % _r, 48, F32)
+for _r in range(3):
+    _b("bc%d" % _r, 256, X4)
+    _b("bs%d" % _r, 256, U8)
+    _b("qs%d" % _r, 128, X4)
+    _b("ss%d" % _r, 128, U8)
+    SCRATCH["fan%d" % _r] = ("dram", [48, 8, 24], F32)
+for _n, _c, _t in (("fp", 4 * C, BF), ("bp", 1024, BF), ("gz", 2 * C, BF), ("zt", 4 * C, BF), ("yt", 4 * C, BF), ("ys", 512, BF), ("yh", 512, BF), ("xsd", 512, BF), ("fh", 256, BF),
+                   ("exs", 40, F32), ("exr", 48, F32), ("lf", 32, F32), ("lw", 32, F32), ("lu", 32, U16), ("mi", 32, U16), ("mu", 32, U16), ("sv", 8, U16), ("lsh", 192, F32),
+                   ("qz", C, X4), ("sz", C, U8), ("qy", C, X4), ("sy", C, U8), ("qys", 128, X4), ("sys0", 128, U8), ("qh", 128, X4), ("sh0", 128, U8),
+                   ("sc", 192, F32), ("fl", 192, F32), ("f1", 96, F32), ("f2", 96, F32), ("f3", 48, F32), ("rk", 32, F32), ("exo", 48, F32),
+                   ("et", 768, BF), ("qe", 192, X4), ("se", 192, U8), ("eq", 192, F32), ("pr", 192, F32), ("p1", 96, F32), ("p2", 48, F32),
+                   ("sg", 32, F32), ("sm", 24, F32), ("s1", 8, F32), ("s2", 8, F32), ("rs", 256, F32), ("yo", C, F32), ("yo2", 64, F32), ("mh", 16, U16),
+                   ("ut", 512, BF), ("vt", 512, BF), ("qu", 128, X4), ("suu", 128, U8), ("qua", 128, X4), ("sua", 128, U8), ("qv", 128, X4), ("svv", 128, U8),
+                   ("wq", 512, X4), ("wsc", 512, U8), ("one", 528, BF), ("wd", 528, BF), ("ce", 512, X4), ("cs", 512, U8), ("ct", 1536, BF), ("cc", 384, X4), ("ccs", 384, U8),
+                   ("pi", 28, I32), ("kk", 128, I32), ("pf", 28, F32), ("pd", 12, F32), ("pe", 12, F32),
+                   ("ip", 16, I32), ("i12", 12, I32), ("cl", 32, F32), ("it", 240, I32), ("ul", 8, U16), ("sl", 4, U16), ("sh", 6, U16), ("shh", 2, U16), ("sd", 6, U16), ("el", 24, U16),
+                   ("q0", 128, F32), ("gk", 192, F32), ("sgn", 96, F32), ("dm", 24, F32), ("on", 32, F32), ("ot", 32, F32)):
+    _b(_n, _c, _t)
+SEMAPHORES = ["kv", "ks", "kt", "kg", "lx", "lp", "lu", "lw", "lv", "st", "loc", "ha0", "ha1", "ha2", "ha3"]
+for _r in range(3):
+    SEMAPHORES += ["se%d" % _r, "ow%d" % _r, "rr%d" % _r, "fw%d" % _r, "fr%d" % _r]
+
+
+def rank_program(g, core, T, topo):
+    rank = T.rank_of(core)
+    if rank is None:
+        return
+    A, F = AluOpType, ActivationFunctionType
+    N = len(T.cores)
+    vec, sca, ten, syn = g.vector, g.scalar, g.tensor, g.sync
+    queue = {"v": vec, "s": sca, "t": ten, "g": g, "y": syn}
+    total, seen, log, hold = {}, {q: {} for q in queue}, {}, []
+
+    def w(name, a, b, step=1, p0=0, p1=128):
+        return (name, a, b, step, p0, p1)
+
+    def ap(v):
+        name, a, b, step, p0, p1 = v
+        t = T[name]
+        if p0 == 0 and p1 == 128:
+            return t[:, a:b] if step == 1 else t[:, a:b:step]
+        return t[p0:p1, a:b] if step == 1 else t[p0:p1, a:b:step]
+
+    def meet(x, y):
+        if x[1] >= y[2] or y[1] >= x[2] or x[4] >= y[5] or y[4] >= x[5]:
+            return False
+        return not (x[3] == y[3] and x[3] > 1 and (x[1] - y[1]) % x[3])
+
+    def wait(q, sem, val):
+        if seen[q].get(sem, 0) < val:
+            queue[q].wait_ge(T.sem[sem], int(val))
+            seen[q][sem] = val
+
+    def order(q, reads, writes, acc, dma):
+        for vs, wr in ((reads, False), (writes, True)):
+            for v in vs:
+                bank = v[0][:2] == "ps"
+                for (o, owr, oq, osem, oval, odma) in log.get(v[0], ()):
+                    if not (bank or meet(v, o)):
+                        continue
+                    if not (wr or owr or (bank and oq != q)):
+                        continue
+                    if oq == q and not odma and not dma:
+                        if (acc and wr) or not owr:
+                            continue
+                    wait(q, osem, total[osem] if odma else oval)
+
+    def note(q, reads, writes, sem, val, dma):
+        for v in writes:
+            old = log.get(v[0], [])
+            log[v[0]] = [e for e in old if not (v[3] == 1 and v[1] <= e[0][1] and v[2] >= e[0][2] and v[4] <= e[0][4] and v[5] >= e[0][5])]
+            log[v[0]].append((v, True, q, sem, val, dma))
+        for v in reads:
+            log.setdefault(v[0], []).append((v, False, q, sem, val, dma))
+
+    def op(q, call, reads, writes, acc=False):
+        if hold:
+            hold[-1].append((q, call, reads, writes, acc))
+            return
+        order(q, reads, writes, acc, False)
+        sem = "k" + q
+        total[sem] = total.get(sem, 0) + 1
+        call().then_inc(T.sem[sem], 1)
+        note(q, reads, writes, sem, total[sem], False)
+
+    def weave(*chains):
+        lists = []
+        for c in chains:
+            hold.append([])
+            c()
+            lists.append(hold.pop())
+        for i in range(max(len(x) for x in lists)):
+            for x in lists:
+                if i < len(x):
+                    op(*x[i])
+
+    def dma(q, out, in_, sem, reads, writes, after=()):
+        order(q, reads, writes, False, True)
+        for s in after:
+            wait(q, s, total[s])
+        total[sem] = total.get(sem, 0) + 16
+        queue[q].dma_start(out, in_).then_inc(T.sem[sem], 16)
+        note(q, reads, writes, sem, total[sem], True)
+
+    def arrive(v, sem, val):
+        total[sem] = val
+        log.setdefault(v[0], []).append((v, True, "r", sem, val, True))
+
+    def at(v, ind):
+        return ap(v) if ind is None else ap(v).indirect(ap(ind))
+
+    def rd(v, ind):
+        return [v] if ind is None else [v, ind]
+
+    def copy(out, in_, ind=None):
+        op("v", lambda: vec.tensor_copy(ap(out), at(in_, ind)), rd(in_, ind), [out])
+
+    def tt(out, a, b, o, ind=None):
+        op("v", lambda: vec.tensor_tensor(ap(out), at(a, ind), ap(b), o), rd(a, ind) + [b], [out])
+
+    def ts(out, a, s1, o1, s2=None, o2=None, ind=None):
+        more = [s for s in (s1, s2) if isinstance(s, tuple)]
+        n1, n2 = [ap(s) if isinstance(s, tuple) else s for s in (s1, s2)]
+        if o2 is None:
+            op("v", lambda: vec.tensor_scalar(ap(out), at(a, ind), n1, None, o1), rd(a, ind) + more, [out])
+        else:
+            op("v", lambda: vec.tensor_scalar(ap(out), at(a, ind), n1, n2, o1, o2), rd(a, ind) + more, [out])
+
+    def fill(out, val):
+        op("v", lambda: vec.memset(ap(out), val), [], [out])
+
+    def act(out, in_, func=None, scale=1.0, ind=None):
+        f = F.Copy if func is None else func
+        if scale == 1.0:
+            op("s", lambda: sca.activation(ap(out), at(in_, ind), f), rd(in_, ind), [out])
+        else:
+            op("s", lambda: sca.activation(ap(out), at(in_, ind), f, scale=scale), rd(in_, ind), [out])
+
+    def quant(q, s, in_):
+        op("v", lambda: vec.quantize_mx(ap(q), ap(s), ap(in_)), [in_], [q, s])
+
+    def mm(out, l, ls, r, rs, start=True, stop=True):
+        op("t", lambda: ten.matmul_mx(ap(out), ap(l), ap(ls), ap(r), ap(rs), start, stop), [l, ls, r, rs], [out], acc=not start)
+
+    def iota(out, pat, base, cm):
+        if SCRATCH[out[0]][2] != I32:
+            op("g", lambda: g.iota(ap(out), pat, base, cm, allow_small_or_imprecise_dtypes=True), [], [out])
+        else:
+            op("g", lambda: g.iota(ap(out), pat, base, cm), [], [out])
+
+    def pick(qo, so, qi, si, ind):
+        op("v", lambda: vec.tensor_copy(ap(qo).bitcast(dt.uint32), ap(qi).bitcast(dt.uint32).indirect(ap(ind))), [qi, ind], [qo])
+        act(so, si, ind=ind)
+
+    up, down = (rank - 1) % N, (rank + 1) % N
+    others = [r for r in range(N) if r != rank]
+
+    def dst(r):
+        rid, pid, _ = topo.addr(T.cores[r])
+        return DstId(rid=rid, pnc=pid)
+
+    def bits(es):
+        return sum(1 << e for e in es)
+
+    def fused(trs, reads):
+        order("g", reads, [], False, True)
+        total["loc"] = total.get("loc", 0) + sum(bin(m).count("1") for _, m, _, _, _ in trs)
+        g.remote_dma_fused([RemoteDMATransfer(dst_ids=ids, dma_engine_mask=m, remote_sem=T.sem[sem], srcs=[src], dsts=dsts) for ids, m, sem, src, dsts in trs], local_sem=T.sem["loc"])
+
+    def halo(k):
+        e, s = "ext%d" % k, "ha%d" % k
+        eu, ed = topo.engines(core, T.cores[up]), topo.engines(core, T.cores[down])
+        hu, hd = eu[:len(eu) // 2], ed[len(ed) // 2:]
+        lo, hi = w(e, 8, 16), w(e, 24, 32)
+        fused([([dst(up)], bits(hu), s, ap(lo), [ap(w(e, 32, 40))]), ([dst(down)], bits(hd), s, ap(hi), [ap(w(e, 0, 8))])], [lo, hi])
+        arrive(w(e, 0, 8), s, len(hu) + len(hd))
+        arrive(w(e, 32, 40), s, len(hu) + len(hd))
+
+    def seeds(k):
+        m = bits(topo.engines(core, T.cores[others[0]]))
+        ids = [dst(r) for r in others]
+        a, b = 64 * rank, 64 * rank + 64
+        q, s, bq, bs = w("qs%d" % k, 0, 64), w("ss%d" % k, 0, 64), w("bc%d" % k, a, b), w("bs%d" % k, a, b)
+        fused([(ids, m, "se%d" % k, ap(q).bitcast(dt.uint8), [ap(bq).bitcast(dt.uint8) for r in others])], [q])
+        fused([(ids, m, "se%d" % k, ap(s), [ap(bs) for r in others])], [s])
+        dma("y", ap(bq).bitcast(dt.uint8), ap(q).bitcast(dt.uint8), "ow%d" % k, [q], [bq])
+        dma("y", ap(bs), ap(s), "ow%d" % k, [s], [bs])
+        n = 2 * len(others) * bin(m).count("1")
+        for r in others:
+            arrive(w("bc%d" % k, 64 * r, 64 * r + 64), "se%d" % k, n)
+            arrive(w("bs%d" % k, 64 * r, 64 * r + 64), "se%d" % k, n)
+
+    def turned(s):
+        for m in range(8):
+            d = s * DC[m]
+            if d == 0:
+                yield m, 0, 16, 0, False
+            elif d > 0:
+                yield m, 0, 16 - d, d, False
+                yield m, 16 - d, 16, 0, True
+            else:
+                yield m, -d, 16, 0, False
+                yield m, 0, -d, 16 + d, True
+
+    dma("y", ap(w("xt0", 0, 4 * C)), T.x[:, :], "lx", [], [w("xt0", 0, 4 * C)])
+    for m, a, b, o, _ in turned(H[0]):
+        v = w("pi", 0, 24, 1, 16 * m + a, 16 * m + b)
+        dma("s", ap(v), T.p[16 * m + o:16 * m + o + b - a, :], "lp", [], [v])
+    dma("y", ap(w("ut", 0, 512)), T.u[:, :], "lu", [], [w("ut", 0, 512)])
+    dma("y", ap(w("wq", 0, 512)).bitcast(dt.uint8), T.wc[:, :], "lw", [], [w("wq", 0, 512)])
+    dma("y", ap(w("wsc", 0, 512)), T.ws[:, :], "lw", [], [w("wsc", 0, 512)])
+    dma("y", ap(w("vt", 0, 512)), T.v[:, :], "lv", [], [w("vt", 0, 512)])
+
+    def ic(i):
+        return w("ip", i, i + 1)
+
+    def fc(i):
+        return w("cl", i, i + 1)
+
+    def it(i, n):
+        return w("it", 12 * i, 12 * i + n)
+
+    P, GI, QI = ic(0), ic(1), ic(2)
+    GF, QF, G16, DR1, CAR, DEL, GX = [fc(i) for i in range(7)]
+    idx, i4, i2 = it(0, 12), it(0, 4), it(0, 2)
+
+    fill(w("one", 0, 515), 1.0)
+    iota(P, [[0, 1]], 0, 1)
+    iota(w("i12", 0, 12), [[16, 12]], 0, 1)
+    op("g", lambda: g.affine_select(ap(w("wd", 0, 515)), ap(w("one", 0, 515)), [[-1, 515]], A.is_equal, 0.0, 3, 4), [w("one", 0, 515)], [w("wd", 0, 515)])
+    iota(w("sgn", 0, 96), [[2, 4], [-1, 8], [0, 3]], 0, 0)
+    iota(w("gk", 0, 192), [[-1, 8], [0, 24]], 0, 0)
+    iota(w("q0", 0, 128), [[0, 8], [1, 16]], 0, 0)
+    iota(w("ct", 0, 512), [[0, 512]], 0, 0)
+
+    ts(GI, P, 4, A.arith_shift_right)
+    ts(QI, P, 15, A.bitwise_and)
+    copy(GF, GI)
+    copy(QF, QI)
+    ts(G16, GF, -16.0, A.mult)
+    ts(idx, w("i12", 0, 12), G16, A.add)
+
+    def c_rows():
+        ts(fc(8), GF, 2.0, A.is_ge)
+        ts(fc(9), GF, 3.0, A.is_ge, fc(8), A.add)
+        tt(DR1, fc(9), fc(11), A.subtract)
+        for i, h in enumerate(H):
+            ts(fc(20 + i), DR1, 2.0 * h, A.mult, 8.0 - 2.0 * h, A.add)
+        ts(w("sh", 0, 2), i2, fc(20), A.add)
+
+    def c_rows2():
+        ts(fc(10), GF, 6.0, A.is_ge)
+        ts(fc(11), GF, 7.0, A.is_ge, fc(10), A.add)
+
+    def c_carry():
+        ts(fc(12), GF, 4.0, A.is_ge)
+        ts(fc(13), GF, 1.0, A.is_ge, fc(12), A.subtract)
+        ts(fc(15), GF, 5.0, A.is_ge)
+        ts(fc(14), QF, float(16 - H[0]), A.is_ge, fc(13), A.mult)
+        ts(fc(16), QF, float(H[0]), A.is_lt, fc(15), A.mult)
+        tt(CAR, fc(14), fc(16), A.add)
+
+    def c_pairs():
+        ts(it(1, 4), i4, 3, A.arith_shift_right, 3, A.bitwise_and)
+        ts(it(2, 4), i4, 5, A.arith_shift_right)
+        ts(it(3, 4), i4, 7, A.bitwise_and)
+        ts(it(1, 4), it(1, 4), 2, A.mult)
+        tt(it(1, 4), it(1, 4), it(2, 4), A.add)
+        tt(it(4, 4), it(1, 4), it(3, 4), A.max)
+        tt(w("it", 52, 56), it(1, 4), it(3, 4), A.min)
+        ts(w("ul", 0, 8), it(4, 8), 16, A.mult)
+
+    def c_half():
+        ts(ic(3), GI, 1, A.bitwise_and)
+        ts(fc(7), ic(3), -2.0, A.mult, 1.0, A.add)
+        tt(GX, fc(7), GF, A.add)
+
+    c_rows2()
+    weave(c_rows, c_carry, c_half)
+
+    def relabel(out, p, n):
+        k = [w("kk", 32 * i, 32 * i + n) for i in range(4)]
+        ts(k[0], p, 7, A.bitwise_and)
+        ts(k[1], k[0], 3, A.mult)
+        ts(k[2], k[1], 7, A.bitwise_and)
+        tt(k[3], k[2], k[0], A.subtract)
+        tt(out, k[3], p, A.add)
+
+    def c_pointers():
+        copy(w("pi", 24, 28), i4)
+        relabel(w("pf", 0, 28), w("pi", 0, 28), 28)
+        tt(w("pd", 0, 12), w("pf", 1, 24, 2), w("pf", 0, 24, 2), A.subtract)
+        ts(w("sl", 0, 4), w("pf", 24, 28), 6.0, A.mult)
+        ts(w("pe", 0, 12), w("pd", 0, 12), CAR, A.mult)
+        tt(w("ext0", 8, 32, 2), w("pf", 0, 24, 2), w("pe", 0, 12), A.add)
+        tt(w("ext0", 9, 32, 2), w("pf", 1, 24, 2), w("pe", 0, 12), A.subtract)
+
+    weave(c_pointers, c_pairs)
+    halo(0)
+
+    quant(w("qx0", 0, C), w("sx0", 0, C), w("xt0", 0, 4 * C))
+    pick(w("qs0", 0, 64), w("ss0", 0, 64), w("qx0", 0, C), w("sx0", 0, C), w("sl", 0, 4))
+    seeds(0)
+    iota(w("et", 0, 768), [[0, 768]], 0, 0)
+    iota(w("dm", 0, 24), [[1, 3], [0, 8]], 0, 0)
+    iota(w("ct", 512, 1536), [[0, 1024]], 0, 0)
+    for b in range(4):
+        quant(w("ce", 128 * b, 128 * b + 128), w("cs", 128 * b, 128 * b + 128), w("wd", 3 - b, 515 - b))
+
+    def bank(b, n, a=0, step=1):
+        return w("ps%d" % b, a, n, step)
+
+    def ceb(b):
+        return w("ce", 128 * b, 128 * b + 128), w("cs", 128 * b, 128 * b + 128)
+
+    def fpw(b, a=0, e=C):
+        return w("fp", C * b + a, C * b + e)
+
+    def unpack_f(k, bs):
+        for b in bs:
+            mm(bank(b, C), *ceb(b), w("qx%d" % k, 0, C), w("sx%d" % k, 0, C))
+            if b < 2:
+                act(fpw(b), bank(b, C))
+
+    unpack_f(0, (0, 1))
+
+    def lists(k, src):
+        copy(w("lf", 0, 32), w(src, 0, 48), w("sh", 2 * k, 2 * k + 2))
+        copy(w("lu", 0, 32), w("lf", 0, 32))
+
+    def fan(k):
+        t = T["fan%d" % k]
+        act(w("lw", 0, 24, 2), w("lf", 1, 24, 2))
+        act(w("lw", 1, 24, 2), w("lf", 0, 24, 2))
+        for j, n in ((1, "lf"), (0, "lw"), (2, "lw")):
+            for m in range(8):
+                v = w(n, 0, 24, 1, 16 * m, 16 * m + 16)
+                dma("y", t[16 * j:16 * j + 16, m, :], ap(v), "fw%d" % k, [v], [])
+        for m in range(8):
+            o = w("lsh", 0, 192, 1, 16 * m, 16 * m + 16)
+            a = 16 + H[k] * DC[m]
+            dma("y", ap(o), t[a:a + 16, :, :], "fr%d" % k, [], [o], ["fw%d" % k])
+
+    def turn(k, s, a, b):
+        e = "ext%d" % (k + 1)
+        act(w("exs", a, b, 2), w(e, a + 1, b, 2))
+        act(w("exs", a + 1, b, 2), w(e, a, b, 2))
+        for m, p, q, o, swap in turned(s):
+            v, d = w("exs" if swap else e, a, b, 1, 16 * m + o, 16 * m + o + q - p), w("exr", a, b, 1, 16 * m + p, 16 * m + q)
+            dma("y", ap(d), ap(v), "rr%d" % k, [v], [d])
+
+    quant(w("qu", 0, 128), w("suu", 0, 128), w("ut", 0, 512))
+    pick(w("qua", 0, 128), w("sua", 0, 128), w("qu", 0, 128), w("suu", 0, 128), w("ul", 0, 8))
+    fill(w("ext0", 40, 48), 0.0)
+
+    def c_spread():
+        n = [it(i, 12) for i in range(6, 13)]
+        ts(n[0], idx, 171, A.mult)
+        ts(n[0], n[0], 12, A.arith_shift_right)
+        ts(n[1], n[0], -24, A.mult)
+        tt(n[1], n[1], idx, A.add)
+        ts(n[2], n[1], 3, A.arith_shift_right)
+        ts(n[3], n[1], 7, A.bitwise_and)
+        ts(n[4], n[0], 3, A.mult, -24, A.add)
+        tt(n[4], n[4], n[2], A.add)
+        ts(n[5], n[3], GF, A.is_equal)
+        ts(n[6], n[3], GX, A.is_equal)
+        tt(n[5], n[5], n[4], A.mult)
+        tt(n[6], n[6], n[4], A.mult)
+        ts(w("el", 0, 12), n[5], 24, A.add)
+        ts(w("el", 12, 24), n[6], 24, A.add)
+
+    def c_misc():
+        ts(w("sgn", 0, 96), w("sgn", 0, 96), 0.0, A.is_ge, 2.0, A.mult)
+        ts(w("gk", 0, 192), w("gk", 0, 192), GF, A.add)
+        ts(w("sgn", 0, 96), w("sgn", 0, 96), -1.0, A.add)
+        fill(w("rk", 24, 32), 0.0)
+
+    def turner(i):
+        h = H[i]
+        for (g0, g1, d, e) in ((0, 1, 0, 0), (1, 4, h, 0), (1, 4, h - 16, 1), (4, 5, 0, 0), (5, 8, -h, 0), (5, 8, 16 - h, 1)):
+            ts(w("ct", 512 * i + 64 * g0 + e, 512 * i + 64 * g1, 4), w("q0", 16 * g0, 16 * g1), float(d), A.add, QF, A.is_equal)
+        quant(w("cc", 128 * i, 128 * i + 128), w("ccs", 128 * i, 128 * i + 128), w("ct", 512 * i, 512 * i + 512))
+
+    def c_seeds():
+        ts(ic(4), P, 15, A.bitwise_and, 1, A.arith_shift_right)
+        ts(it(13, 2), i2, 7, A.bitwise_and)
+        ts(ic(5), ic(4), 11, A.mult)
+        ts(it(14, 2), i2, 3, A.arith_shift_right)
+        ts(ic(5), ic(5), 5, A.arith_shift_right)
+        ts(it(13, 2), it(13, 2), 3, A.mult)
+        ts(ic(5), ic(5), -3, A.mult)
+        tt(it(13, 2), it(13, 2), it(14, 2), A.add)
+        tt(DEL, ic(5), ic(4), A.add)
+        for i in range(2):
+            ts(w("sd", 2 * i, 2 * i + 2), it(13, 2), fc(20 + i), A.add)
+        ts(w("dm", 0, 24), w("dm", 0, 24), DEL, A.is_equal)
+
+    weave(c_spread, c_misc)
+    lists(0, "ext0")
+    fan(0)
+    turner(0)
+
+    def bwin(b):
+        return w("bp", 256 * b, 256 * b + 256)
+
+    def wb(b):
+        return w("wq", 128 * b, 128 * b + 128), w("wsc", 128 * b, 128 * b + 128)
+
+    def gather(out, b, ind):
+        if b < 2:
+            ts(out, bwin(b), 0.015625, A.mult, ind=ind)
+        else:
+            act(out, bwin(b), scale=0.015625, ind=ind)
+
+    for k in range(3):
+        h, last = H[k], k == 2
+        e = "ext%d" % (k + 1)
+        lu, sv = w("lu", 0, 24), w("sv", 0, 8)
+        sh = w("sh", 2 * k, 2 * k + 2)
+
+        def unpack_b(b):
+            mm(bank(4 + b, 256), *ceb(b), w("bc%d" % k, 0, 256), w("bs%d" % k, 0, 256))
+            if b < 2:
+                copy(bwin(b), bank(4 + b, 256))
+            else:
+                act(bwin(b), bank(4 + b, 256))
+
+        def z_of(b):
+            z, gz = w("zt", b, 4 * C, 4), w("gz", C * (b % 2), C * (b % 2) + C)
+            if b < 2:
+                tt(z, bwin(b), fpw(b), A.subtract, ind=lu)
+            else:
+                act(gz, bwin(b), ind=lu)
+                tt(z, gz, bank(b, C), A.subtract)
+
+        unpack_b(0)
+        z_of(0)
+        unpack_b(2)
+        unpack_b(1)
+        unpack_f(k, (2,))
+        z_of(2)
+        unpack_b(3)
+        unpack_f(k, (3,))
+        z_of(1)
+        z_of(3)
+        for t in range(3):
+            qz, sz = w("qz", 128 * t, 128 * t + 128), w("sz", 128 * t, 128 * t + 128)
+            quant(qz, sz, w("zt", 512 * t, 512 * t + 512))
+            mm(bank(4 + t, 128), qz, sz, w("qua", 0, 128), w("sua", 0, 128))
+            act(w("sc", 64 * t, 64 * t + 64), bank(4 + t, 128, 64))
+        for t in range(3):
+            tt(w("fl", t, 192, 3), bank(4 + t, 64), w("sc", 64 * t, 64 * t + 64), A.is_gt)
+        tt(w("f1", 0, 96), w("fl", 0, 96), w("fl", 96, 192), A.add)
+        tt(w("f2", 0, 96), w("f1", 0, 96), w("sgn", 0, 96), A.mult)
+        tt(w("f3", 0, 48), w("f2", 0, 48), w("f2", 48, 96), A.add)
+        tt(w("rk", 0, 24), w("f3", 0, 24), w("f3", 24, 48), A.add)
+        copy(w("et", 0, 768, 4), w("rk", 0, 32), w("el", 0, 12))
+        act(w("et", 1, 768, 4), w("rk", 0, 32), ind=w("el", 12, 24))
+        quant(w("qe", 0, 192), w("se", 0, 192), w("et", 0, 768))
+        mm(bank(7, 192), w("cc", 128 * k, 128 * k + 128), w("ccs", 128 * k, 128 * k + 128), w("qe", 0, 192), w("se", 0, 192))
+        for b in (2, 3):
+            act(fpw(b), bank(b, C))
+        tt(w("eq", 0, 192), bank(7, 192), w("gk", 0, 192), A.is_equal)
+        tt(w("pr", 0, 192), w("eq", 0, 192), w("lsh", 0, 192), A.mult)
+        tt(w("p1", 0, 96), w("pr", 0, 96), w("pr", 96, 192), A.add)
+        tt(w("p2", 0, 48), w("p1", 0, 48), w("p1", 48, 96), A.add)
+        tt(w(e, 8, 32), w("p2", 0, 24), w("p2", 24, 48), A.add)
+        halo(k + 1)
+        if last:
+            turn(k, -h, 8, 32)
+            for b in range(4):
+                act(w("fh", 64 * b, 64 * b + 32), fpw(b, 0, 32))
+                act(w("fh", 64 * b + 32, 64 * b + 64), fpw(b, 352, 384))
+        if k == 0:
+            fill(w("exo", 0, 48), 0.0)
+            weave(c_seeds)
+            for i in range(1, 4):
+                fill(w("ext%d" % i, 40, 48), 0.0)
+            fill(w("exr", 40, 48), 0.0)
+            for i in (1, 2):
+                ts(w("sh", 2 * i, 2 * i + 2), i2, fc(20 + i), A.add)
+            fill(w("xsd", 256, 512), 0.0)
+        tt(w("exo", 8, 32), w("p2", 0, 24), w("p2", 24, 48), A.add)
+        copy(w("mi", 0, 32), w("exo", 0, 48), sh)
+        a, z = 32 * h, C - 32 * h
+        for b in (0, 2, 1, 3):
+            gather(w("yt", 4 * a + b, 4 * z, 4), b, w("mi", a // 16, z // 16))
+        if k == 0:
+            turner(1)
+        if not last:
+            turn(k, H[k + 1] - h, 0, 40)
+            copy(w("sg", 0, 32), w(e, 0, 48), w("sd", 2 * k, 2 * k + 2))
+            tt(w("sm", 0, 24), w("sg", 0, 24), w("dm", 0, 24), A.mult)
+            tt(w("s1", 0, 8), w("sm", 0, 8), w("sm", 8, 16), A.add)
+            tt(w("s2", 0, 8), w("s1", 0, 8), w("sm", 16, 24), A.add)
+            copy(sv, w("s2", 0, 8))
+            for b in (0, 2, 1, 3):
+                gather(w("ys", b, 512, 4), b, sv)
+            quant(w("qys", 0, 128), w("sys0", 0, 128), w("ys", 0, 512))
+            for b in range(4):
+                mm(bank(b, 128), *wb(b), w("qys", 0, 128), w("sys0", 0, 128))
+                act(w("rs", 64 * b, 64 * b + 64), bank(b, 128, 0, 2), F.Relu)
+            copy(w("mu", 0, 32), w(e, 0, 48), sh)
+            for b in range(4):
+                tt(w("xsd", b, 256, 4), w("rs", 64 * b, 64 * b + 64), w("bp", 256 * b + 64 * rank, 256 * b + 64 * rank + 64), A.add)
+            quant(w("qs%d" % (k + 1), 0, 128), w("ss%d" % (k + 1), 0, 128), w("xsd", 0, 512))
+            seeds(k + 1)
+            for b in (0, 2, 1, 3):
+                gather(w("yt", b, 4 * a, 4), b, w("mu", 0, a // 16))
+                gather(w("yt", 4 * z + b, 4 * C, 4), b, w("mu", z // 16, 24))
+            a, z = 0, C
+        xn, n = "xt%d" % (k + 1), z - a
+        qy, sy = w("qy", a, z), w("sy", a, z)
+        quant(qy, sy, w("yt", 4 * a, 4 * z))
+        for b in range(4):
+            mm(bank(4 + b, n), *ceb(b), w("qx%d" % k, a, z), w("sx%d" % k, a, z), True, False)
+        for b in range(4):
+            mm(bank(4 + b, n), *wb(b), qy, sy, False, True)
+            tt(w(xn, 4 * a + b, 4 * z, 4), bank(4 + b, n), fpw(b, a, z), A.max)
+        if not last:
+            lists(k + 1, "exr")
+        quant(w("qx%d" % (k + 1), a, z), w("sx%d" % (k + 1), a, z), w(xn, 4 * a, 4 * z))
+        if not last:
+            unpack_f(k + 1, (0, 1))
+            fan(k + 1)
+        if k == 0:
+            fill(w("yh", 256, 512), 0.0)
+        if k == 1:
+            quant(w("qv", 0, 128), w("svv", 0, 128), w("vt", 0, 512))
+            ts(it(15, 1), it(0, 1), 2, A.is_ge, 20, A.mult)
+            tt(it(15, 1), it(15, 1), it(0, 1), A.add)
+            ts(w("shh", 0, 1), it(15, 1), fc(22), A.add)
+            turner(2)
+
+    qv, svv = w("qv", 0, 128), w("svv", 0, 128)
+    x3, s3 = w("qx3", 32, 352), w("sx3", 32, 352)
+    mm(bank(4, 320), qv, svv, x3, s3)
+    act(w("yo", 32, 352), bank(4, 320))
+
+    def out_scales(c0, c1, name, a, b):
+        for i in range(4):
+            dma("y", T.osc[4 * i:4 * i + 4, c0:c1], ap(w(name, a, b, 1, 32 * i, 32 * i + 4)), "st", [w(name, a, b)], [])
+
+    copy(w("mh", 0, 16), w("ext3", 0, 48), w("shh", 0, 1))
+    for b in (0, 2, 1, 3):
+        gather(w("yh", b, 256, 4), b, w("mh", 0, 4))
+    quant(w("qys", 0, 128), w("sys0", 0, 128), w("yh", 0, 512))
+    for b in range(4):
+        mm(bank(b, 128), *wb(b), w("qys", 0, 128), w("sys0", 0, 128))
+        act(w("rs", 64 * b, 64 * b + 64), bank(b, 64), F.Relu)
+    for b in range(4):
+        tt(w("xsd", b, 256, 4), w("rs", 64 * b, 64 * b + 64), w("fh", 64 * b, 64 * b + 64), A.add)
+    quant(w("qh", 0, 128), w("sh0", 0, 128), w("xsd", 0, 512))
+    mm(bank(7, 128), qv, svv, w("qh", 0, 128), w("sh0", 0, 128))
+    act(w("yo2", 0, 64), bank(7, 64))
+    pn = w("pi", 0, 24)
+    fill(w("on", 24, 32), 0.0)
+    copy(pn, w("exr", 8, 32))
+    relabel(w("on", 0, 24), pn, 24)
+    op("v", lambda: vec.transpose(ap(w("ot", 0, 32)), ap(w("on", 0, 32))), [w("on", 0, 32)], [w("ot", 0, 32)])
+    dma("y", T.oc[:, 128:1408], ap(x3).bitcast(dt.uint8), "st", [x3], [])
+    out_scales(32, 352, "sx3", 32, 352)
+    dma("y", T.y[:, 32:352], ap(w("yo", 32, 352)), "st", [w("yo", 32, 352)], [])
+    for a, b in ((0, 0), (32, 352)):
+        v = w("qh", a, a + 32)
+        dma("y", T.oc[:, 4 * b:4 * b + 128], ap(v).bitcast(dt.uint8), "st", [v], [])
+        out_scales(b, b + 32, "sh0", a, a + 32)
+        v = w("yo2", a, a + 32)
+        dma("s", T.y[:, b:b + 32], ap(v), "st", [v], [])
+    for m in range(8):
+        v = w("ot", 16 * (m % 2), 16 * (m % 2) + 16, 1, 32 * (m // 2), 32 * (m // 2) + 24)
+        dma("y", T.op[m:m + 1, :], ap(v), "st", [v], [])
+    for sem in SEMAPHORES:
+        if total.get(sem, 0):
+            wait("g", sem, total[sem])

@@ -4,6 +4,8 @@ from concourse.mybir import dt, AluOpType, ActivationFunctionType
 C = 384
 H = [4, 2, 1]
 DC = [0, 1, 1, 1, 0, -1, -1, -1]
+SG, VG = (0, 1), (2, 3)
+BIG = 512.0
 
 SCRATCH = {}
 
@@ -19,26 +21,28 @@ for _r in range(4):
     _b("xt%d" % _r, 4 * C, BF)
     _b("qx%d" % _r, C, X4)
     _b("sx%d" % _r, C, U8)
-    _b("ext%d" % _r, 48, F32)
+    _b("ext%d" % _r, 40, F32)
 for _r in range(3):
     _b("bc%d" % _r, 256, X4)
     _b("bs%d" % _r, 256, U8)
     _b("qs%d" % _r, 128, X4)
     _b("ss%d" % _r, 128, U8)
+    _b("qf%d" % _r, 128, X4)
+    _b("sf%d" % _r, 128, U8)
     SCRATCH["fan%d" % _r] = ("dram", [48, 8, 24], F32)
-for _n, _c, _t in (("fp", 4 * C, BF), ("bp", 1024, BF), ("gz", 2 * C, BF), ("zt", 4 * C, BF), ("yt", 4 * C, BF), ("ys", 512, BF), ("yh", 512, BF), ("xsd", 512, BF), ("fh", 256, BF),
-                   ("exs", 40, F32), ("exr", 48, F32), ("lf", 32, F32), ("lw", 32, F32), ("lu", 32, U16), ("mi", 32, U16), ("mu", 32, U16), ("sv", 8, U16), ("lsh", 192, F32),
-                   ("qz", C, X4), ("sz", C, U8), ("qy", C, X4), ("sy", C, U8), ("qys", 128, X4), ("sys0", 128, U8), ("qh", 128, X4), ("sh0", 128, U8),
-                   ("sc", 192, F32), ("fl", 192, F32), ("f1", 96, F32), ("f2", 96, F32), ("f3", 48, F32), ("rk", 32, F32), ("exo", 48, F32),
-                   ("et", 768, BF), ("qe", 192, X4), ("se", 192, U8), ("eq", 192, F32), ("pr", 192, F32), ("p1", 96, F32), ("p2", 48, F32),
-                   ("sg", 32, F32), ("sm", 24, F32), ("s1", 8, F32), ("s2", 8, F32), ("rs", 256, F32), ("yo", C, F32), ("yo2", 64, F32), ("mh", 16, U16),
+for _n, _c, _t in (("fp", 4 * C, BF), ("bp", 1024, BF), ("gz", 2 * C, BF), ("zt", 4 * C, BF), ("yt", 4 * C, BF), ("ys", 512, BF), ("yh", 512, BF), ("xsd", 512, BF), ("xhd", 512, BF), ("fh", 256, BF),
+                   ("exs", 40, F32), ("exr", 40, F32), ("lf", 32, F32), ("lw", 24, F32), ("lu", 32, U16), ("mi", 32, U16), ("mu", 32, U16), ("sv", 8, U16), ("lsh", 192, F32), ("lsp", 192, F32),
+                   ("qz", C, X4), ("sz", C, U8), ("qy", C, X4), ("sy", C, U8), ("qys", 128, X4), ("sys0", 128, U8), ("qyh", 128, X4), ("syh", 128, U8), ("qh", 128, X4), ("sh0", 128, U8),
+                   ("sc", 192, F32), ("fl", 192, F32), ("rr", 88, F32), ("rk", 200, F32), ("exo", 40, F32),
+                   ("et", 768, BF), ("qe", 192, X4), ("se", 192, U8), ("un", 192, BF), ("cl2", 192, BF), ("r2", 192, BF), ("np", 192, F32),
+                   ("sm", 32, F32), ("s2", 24, F32), ("yo", C, F32), ("yo2", 64, F32), ("mh", 16, U16),
                    ("ut", 512, BF), ("vt", 512, BF), ("qu", 128, X4), ("suu", 128, U8), ("qua", 128, X4), ("sua", 128, U8), ("qv", 128, X4), ("svv", 128, U8),
                    ("wq", 512, X4), ("wsc", 512, U8), ("one", 528, BF), ("wd", 528, BF), ("ce", 512, X4), ("cs", 512, U8), ("ct", 1536, BF), ("cc", 384, X4), ("ccs", 384, U8),
-                   ("pi", 28, I32), ("kk", 128, I32), ("pf", 28, F32), ("pd", 12, F32), ("pe", 12, F32),
-                   ("ip", 16, I32), ("i12", 12, I32), ("cl", 32, F32), ("it", 240, I32), ("ul", 8, U16), ("sl", 4, U16), ("sh", 6, U16), ("shh", 2, U16), ("sd", 6, U16), ("el", 24, U16),
-                   ("q0", 128, F32), ("gk", 192, F32), ("sgn", 96, F32), ("dm", 24, F32), ("on", 32, F32), ("ot", 32, F32)):
+                   ("pi", 40, I32), ("po", 24, I32), ("kk", 160, I32), ("pf", 40, F32), ("pd", 20, F32), ("pe", 20, F32),
+                   ("ip", 16, I32), ("i12", 12, I32), ("cl", 32, F32), ("it", 240, I32), ("ul", 20, U16), ("sh", 6, U16), ("shh", 2, U16), ("el", 36, U16),
+                   ("q0", 128, F32), ("dm", 33, F32), ("on", 32, F32), ("ot", 32, F32)):
     _b(_n, _c, _t)
-SEMAPHORES = ["kv", "ks", "kt", "kg", "lx", "lp", "lu", "lw", "lv", "st", "loc", "ha0", "ha1", "ha2", "ha3"]
+SEMAPHORES = ["kv", "ks", "kt", "kg", "lx", "lp", "lu", "lw", "lv", "st", "eg", "loc", "ha0", "ha1", "ha2", "ha3"]
 for _r in range(3):
     SEMAPHORES += ["se%d" % _r, "ow%d" % _r, "rr%d" % _r, "fw%d" % _r, "fr%d" % _r]
 
@@ -105,16 +109,23 @@ def rank_program(g, core, T, topo):
         call().then_inc(T.sem[sem], 1)
         note(q, reads, writes, sem, total[sem], False)
 
+    def calls(c):
+        hold.append([])
+        c()
+        return hold.pop()
+
     def weave(*chains):
-        lists = []
-        for c in chains:
-            hold.append([])
-            c()
-            lists.append(hold.pop())
+        lists = [calls(c) for c in chains]
         for i in range(max(len(x) for x in lists)):
             for x in lists:
                 if i < len(x):
                     op(*x[i])
+
+    spare = []
+
+    def idle(n):
+        for _ in range(min(n, len(spare))):
+            op(*spare.pop(0))
 
     def dma(q, out, in_, sem, reads, writes, after=()):
         order(q, reads, writes, False, True)
@@ -148,15 +159,19 @@ def rank_program(g, core, T, topo):
         else:
             op("v", lambda: vec.tensor_scalar(ap(out), at(a, ind), n1, n2, o1, o2), rd(a, ind) + more, [out])
 
+    def scan(out, d0, d1):
+        op("v", lambda: vec.tensor_tensor_scan(ap(out), ap(d0), ap(d1), 0.0, A.mult, A.add), [d0, d1], [out])
+
     def fill(out, val):
         op("v", lambda: vec.memset(ap(out), val), [], [out])
 
-    def act(out, in_, func=None, scale=1.0, ind=None):
-        f = F.Copy if func is None else func
-        if scale == 1.0:
-            op("s", lambda: sca.activation(ap(out), at(in_, ind), f), rd(in_, ind), [out])
+    def act(out, in_, scale=1.0, ind=None, bias=None):
+        if bias is not None:
+            op("s", lambda: sca.activation(ap(out), at(in_, ind), F.Identity, bias=ap(bias)), rd(in_, ind) + [bias], [out])
+        elif scale == 1.0:
+            op("s", lambda: sca.activation(ap(out), at(in_, ind), F.Copy), rd(in_, ind), [out])
         else:
-            op("s", lambda: sca.activation(ap(out), at(in_, ind), f, scale=scale), rd(in_, ind), [out])
+            op("s", lambda: sca.activation(ap(out), at(in_, ind), F.Copy, scale=scale), rd(in_, ind), [out])
 
     def quant(q, s, in_):
         op("v", lambda: vec.quantize_mx(ap(q), ap(s), ap(in_)), [in_], [q, s])
@@ -189,8 +204,8 @@ def rank_program(g, core, T, topo):
         total["loc"] = total.get("loc", 0) + sum(bin(m).count("1") for _, m, _, _, _ in trs)
         g.remote_dma_fused([RemoteDMATransfer(dst_ids=ids, dma_engine_mask=m, remote_sem=T.sem[sem], srcs=[src], dsts=dsts) for ids, m, sem, src, dsts in trs], local_sem=T.sem["loc"])
 
-    def halo(k):
-        e, s = "ext%d" % k, "ha%d" % k
+    def halo(k, e):
+        s = "ha%d" % k
         eu, ed = topo.engines(core, T.cores[up]), topo.engines(core, T.cores[down])
         hu, hd = eu[:len(eu) // 2], ed[len(ed) // 2:]
         lo, hi = w(e, 8, 16), w(e, 24, 32)
@@ -224,10 +239,10 @@ def rank_program(g, core, T, topo):
                 yield m, -d, 16, 0, False
                 yield m, 0, -d, 16 + d, True
 
-    dma("y", ap(w("xt0", 0, 4 * C)), T.x[:, :], "lx", [], [w("xt0", 0, 4 * C)])
     for m, a, b, o, _ in turned(H[0]):
-        v = w("pi", 0, 24, 1, 16 * m + a, 16 * m + b)
+        v = w("pi", 8, 32, 1, 16 * m + a, 16 * m + b)
         dma("s", ap(v), T.p[16 * m + o:16 * m + o + b - a, :], "lp", [], [v])
+    dma("y", ap(w("xt0", 0, 4 * C)), T.x[:, :], "lx", [], [w("xt0", 0, 4 * C)])
     dma("y", ap(w("ut", 0, 512)), T.u[:, :], "lu", [], [w("ut", 0, 512)])
     dma("y", ap(w("wq", 0, 512)).bitcast(dt.uint8), T.wc[:, :], "lw", [], [w("wq", 0, 512)])
     dma("y", ap(w("wsc", 0, 512)), T.ws[:, :], "lw", [], [w("wsc", 0, 512)])
@@ -244,16 +259,23 @@ def rank_program(g, core, T, topo):
 
     P, GI, QI = ic(0), ic(1), ic(2)
     GF, QF, G16, DR1, CAR, DEL, GX = [fc(i) for i in range(7)]
-    idx, i4, i2 = it(0, 12), it(0, 4), it(0, 2)
+    MG, NG, FX = fc(24), fc(25), fc(26)
+    idx, i8, i4, i2 = it(0, 12), it(0, 8), it(0, 4), it(0, 2)
+    LU, LH, LS, LP = w("ul", 0, 8), w("ul", 8, 16), w("ul", 16, 20), w("el", 24, 36)
+    R1, R3 = w("rr", 0, 64), w("rr", 64, 88)
 
     fill(w("one", 0, 515), 1.0)
     iota(P, [[0, 1]], 0, 1)
     iota(w("i12", 0, 12), [[16, 12]], 0, 1)
     op("g", lambda: g.affine_select(ap(w("wd", 0, 515)), ap(w("one", 0, 515)), [[-1, 515]], A.is_equal, 0.0, 3, 4), [w("one", 0, 515)], [w("wd", 0, 515)])
-    iota(w("sgn", 0, 96), [[2, 4], [-1, 8], [0, 3]], 0, 0)
-    iota(w("gk", 0, 192), [[-1, 8], [0, 24]], 0, 0)
     iota(w("q0", 0, 128), [[0, 8], [1, 16]], 0, 0)
-    iota(w("ct", 0, 512), [[0, 512]], 0, 0)
+    halo(0, "pi")
+
+    def zeros(v):
+        act(v, w("one", 0, v[2] - v[1]), scale=0.0)
+
+    for v in (w("ct", 0, 512), w("exo", 0, 40), w("xsd", 256, 512), w("yh", 256, 512), w("xhd", 256, 512)):
+        zeros(v)
 
     ts(GI, P, 4, A.arith_shift_right)
     ts(QI, P, 15, A.bitwise_and)
@@ -262,17 +284,32 @@ def rank_program(g, core, T, topo):
     ts(G16, GF, -16.0, A.mult)
     ts(idx, w("i12", 0, 12), G16, A.add)
 
+    def relabel(out, p, n):
+        k = [w("kk", 40 * i, 40 * i + n) for i in range(4)]
+        ts(k[0], p, 7, A.bitwise_and)
+        ts(k[1], k[0], 3, A.mult)
+        ts(k[2], k[1], 7, A.bitwise_and)
+        tt(k[3], k[2], k[0], A.subtract)
+        tt(out, k[3], p, A.add)
+
+    def c_own():
+        relabel(it(17, 4), i4, 4)
+        ts(LS, it(17, 4), 6.0, A.mult)
+
     def c_rows():
         ts(fc(8), GF, 2.0, A.is_ge)
         ts(fc(9), GF, 3.0, A.is_ge, fc(8), A.add)
         tt(DR1, fc(9), fc(11), A.subtract)
         for i, h in enumerate(H):
             ts(fc(20 + i), DR1, 2.0 * h, A.mult, 8.0 - 2.0 * h, A.add)
-        ts(w("sh", 0, 2), i2, fc(20), A.add)
+        for i in range(3):
+            ts(w("sh", 2 * i, 2 * i + 2), i2, 23.0, A.min, fc(20 + i), A.add)
 
     def c_rows2():
         ts(fc(10), GF, 6.0, A.is_ge)
         ts(fc(11), GF, 7.0, A.is_ge, fc(10), A.add)
+        ts(it(18, 8), i8, 1, A.arith_shift_right)
+        ts(LH, it(18, 8), 0, A.add)
 
     def c_carry():
         ts(fc(12), GF, 4.0, A.is_ge)
@@ -283,50 +320,42 @@ def rank_program(g, core, T, topo):
         tt(CAR, fc(14), fc(16), A.add)
 
     def c_pairs():
-        ts(it(1, 4), i4, 3, A.arith_shift_right, 3, A.bitwise_and)
-        ts(it(2, 4), i4, 5, A.arith_shift_right)
+        ts(it(1, 4), i4, 3, A.arith_shift_right)
         ts(it(3, 4), i4, 7, A.bitwise_and)
-        ts(it(1, 4), it(1, 4), 2, A.mult)
-        tt(it(1, 4), it(1, 4), it(2, 4), A.add)
         tt(it(4, 4), it(1, 4), it(3, 4), A.max)
         tt(w("it", 52, 56), it(1, 4), it(3, 4), A.min)
-        ts(w("ul", 0, 8), it(4, 8), 16, A.mult)
+        ts(LU, it(4, 8), 16, A.mult)
 
     def c_half():
         ts(ic(3), GI, 1, A.bitwise_and)
         ts(fc(7), ic(3), -2.0, A.mult, 1.0, A.add)
         tt(GX, fc(7), GF, A.add)
+        ts(MG, GF, BIG, A.mult)
+        ts(NG, GF, -BIG, A.mult)
+        ts(FX, GF, 256.0, A.mult, -7.0 * 256.0, A.add)
 
-    c_rows2()
+    def c_ones():
+        fill(R1, 1.0)
+        ts(w("rr", 0, 64, 8), w("rr", 0, 64, 8), 0.0, A.mult)
+        ts(w("rr", 9, 64, 9), w("rr", 9, 64, 9), -1.0, A.mult)
+        fill(w("rk", 192, 200), 0.0)
+
+    def c_ones2():
+        fill(w("r2", 0, 192), 1.0)
+        ts(w("r2", 0, 192, 8), w("r2", 0, 192, 8), 0.0, A.mult)
+        fill(R3, 1.0)
+        ts(w("rr", 64, 88, 3), w("rr", 64, 88, 3), 0.0, A.mult)
+
+    weave(c_rows2, c_own, c_pairs)
     weave(c_rows, c_carry, c_half)
 
-    def relabel(out, p, n):
-        k = [w("kk", 32 * i, 32 * i + n) for i in range(4)]
-        ts(k[0], p, 7, A.bitwise_and)
-        ts(k[1], k[0], 3, A.mult)
-        ts(k[2], k[1], 7, A.bitwise_and)
-        tt(k[3], k[2], k[0], A.subtract)
-        tt(out, k[3], p, A.add)
-
-    def c_pointers():
-        copy(w("pi", 24, 28), i4)
-        relabel(w("pf", 0, 28), w("pi", 0, 28), 28)
-        tt(w("pd", 0, 12), w("pf", 1, 24, 2), w("pf", 0, 24, 2), A.subtract)
-        ts(w("sl", 0, 4), w("pf", 24, 28), 6.0, A.mult)
-        ts(w("pe", 0, 12), w("pd", 0, 12), CAR, A.mult)
-        tt(w("ext0", 8, 32, 2), w("pf", 0, 24, 2), w("pe", 0, 12), A.add)
-        tt(w("ext0", 9, 32, 2), w("pf", 1, 24, 2), w("pe", 0, 12), A.subtract)
-
-    weave(c_pointers, c_pairs)
-    halo(0)
-
     quant(w("qx0", 0, C), w("sx0", 0, C), w("xt0", 0, 4 * C))
-    pick(w("qs0", 0, 64), w("ss0", 0, 64), w("qx0", 0, C), w("sx0", 0, C), w("sl", 0, 4))
+    pick(w("qs0", 0, 64), w("ss0", 0, 64), w("qx0", 0, C), w("sx0", 0, C), LS)
     seeds(0)
+    iota(w("dm", 0, 33), [[0, 11], [1, 3]], 0, 0)
     iota(w("et", 0, 768), [[0, 768]], 0, 0)
-    iota(w("dm", 0, 24), [[1, 3], [0, 8]], 0, 0)
     iota(w("ct", 512, 1536), [[0, 1024]], 0, 0)
-    for b in range(4):
+    for b in VG + SG:
         quant(w("ce", 128 * b, 128 * b + 128), w("cs", 128 * b, 128 * b + 128), w("wd", 3 - b, 515 - b))
 
     def bank(b, n, a=0, step=1):
@@ -338,17 +367,26 @@ def rank_program(g, core, T, topo):
     def fpw(b, a=0, e=C):
         return w("fp", C * b + a, C * b + e)
 
-    def unpack_f(k, bs):
-        for b in bs:
-            mm(bank(b, C), *ceb(b), w("qx%d" % k, 0, C), w("sx%d" % k, 0, C))
-            if b < 2:
-                act(fpw(b), bank(b, C))
+    def mm_f(k, b):
+        mm(bank(b, C), *ceb(b), w("qx%d" % k, 0, C), w("sx%d" % k, 0, C))
 
-    unpack_f(0, (0, 1))
+    for b in VG + SG:
+        mm_f(0, b)
+    for b in VG:
+        act(fpw(b), bank(b, C))
+
+    def c_pointers():
+        relabel(w("pf", 0, 40), w("pi", 0, 40), 40)
+        tt(w("pd", 0, 20), w("pf", 1, 40, 2), w("pf", 0, 40, 2), A.subtract)
+        ts(w("pe", 0, 20), w("pd", 0, 20), CAR, A.mult)
+        tt(w("ext0", 0, 40, 2), w("pf", 0, 40, 2), w("pe", 0, 20), A.add)
+        tt(w("ext0", 1, 40, 2), w("pf", 1, 40, 2), w("pe", 0, 20), A.subtract)
 
     def lists(k, src):
-        copy(w("lf", 0, 32), w(src, 0, 48), w("sh", 2 * k, 2 * k + 2))
-        copy(w("lu", 0, 32), w("lf", 0, 32))
+        act(w("lf", 0, 32), w(src, 0, 40), ind=w("sh", 2 * k, 2 * k + 2), bias=MG)
+
+    def list_u(k, src):
+        copy(w("lu", 0, 32), w(src, 0, 40), w("sh", 2 * k, 2 * k + 2))
 
     def fan(k):
         t = T["fan%d" % k]
@@ -367,36 +405,35 @@ def rank_program(g, core, T, topo):
         e = "ext%d" % (k + 1)
         act(w("exs", a, b, 2), w(e, a + 1, b, 2))
         act(w("exs", a + 1, b, 2), w(e, a, b, 2))
-        for m, p, q, o, swap in turned(s):
+        for m, p, q, o, swap in sorted(turned(s), key=lambda x: x[4]):
             v, d = w("exs" if swap else e, a, b, 1, 16 * m + o, 16 * m + o + q - p), w("exr", a, b, 1, 16 * m + p, 16 * m + q)
             dma("y", ap(d), ap(v), "rr%d" % k, [v], [d])
 
-    quant(w("qu", 0, 128), w("suu", 0, 128), w("ut", 0, 512))
-    pick(w("qua", 0, 128), w("sua", 0, 128), w("qu", 0, 128), w("suu", 0, 128), w("ul", 0, 8))
-    fill(w("ext0", 40, 48), 0.0)
-
     def c_spread():
         n = [it(i, 12) for i in range(6, 13)]
-        ts(n[0], idx, 171, A.mult)
-        ts(n[0], n[0], 12, A.arith_shift_right)
-        ts(n[1], n[0], -24, A.mult)
-        tt(n[1], n[1], idx, A.add)
-        ts(n[2], n[1], 3, A.arith_shift_right)
+        ts(n[0], idx, 7, A.bitwise_and)
+        ts(n[1], idx, 3, A.arith_shift_right)
+        ts(n[2], n[1], 24, A.bitwise_and)
         ts(n[3], n[1], 7, A.bitwise_and)
-        ts(n[4], n[0], 3, A.mult, -24, A.add)
-        tt(n[4], n[4], n[2], A.add)
+        tt(n[4], n[0], n[2], A.add)
+        ts(n[4], n[4], 8, A.mult, 7 - 192, A.add)
         ts(n[5], n[3], GF, A.is_equal)
         ts(n[6], n[3], GX, A.is_equal)
         tt(n[5], n[5], n[4], A.mult)
         tt(n[6], n[6], n[4], A.mult)
-        ts(w("el", 0, 12), n[5], 24, A.add)
-        ts(w("el", 12, 24), n[6], 24, A.add)
+        ts(w("el", 0, 12), n[5], 192, A.add)
+        ts(w("el", 12, 24), n[6], 192, A.add)
+        ts(n[2], n[0], 24, A.mult)
+        tt(n[2], n[2], n[1], A.add)
+        ts(LP, n[2], 0, A.add)
 
-    def c_misc():
-        ts(w("sgn", 0, 96), w("sgn", 0, 96), 0.0, A.is_ge, 2.0, A.mult)
-        ts(w("gk", 0, 192), w("gk", 0, 192), GF, A.add)
-        ts(w("sgn", 0, 96), w("sgn", 0, 96), -1.0, A.add)
-        fill(w("rk", 24, 32), 0.0)
+    def c_seeds():
+        ts(ic(4), QI, 1, A.arith_shift_right)
+        ts(ic(5), ic(4), 11, A.mult)
+        ts(ic(5), ic(5), 5, A.arith_shift_right)
+        ts(ic(5), ic(5), -3, A.mult)
+        tt(DEL, ic(5), ic(4), A.add)
+        ts(w("dm", 0, 33), w("dm", 0, 33), DEL, A.is_equal)
 
     def turner(i):
         h = H[i]
@@ -404,24 +441,20 @@ def rank_program(g, core, T, topo):
             ts(w("ct", 512 * i + 64 * g0 + e, 512 * i + 64 * g1, 4), w("q0", 16 * g0, 16 * g1), float(d), A.add, QF, A.is_equal)
         quant(w("cc", 128 * i, 128 * i + 128), w("ccs", 128 * i, 128 * i + 128), w("ct", 512 * i, 512 * i + 512))
 
-    def c_seeds():
-        ts(ic(4), P, 15, A.bitwise_and, 1, A.arith_shift_right)
-        ts(it(13, 2), i2, 7, A.bitwise_and)
-        ts(ic(5), ic(4), 11, A.mult)
-        ts(it(14, 2), i2, 3, A.arith_shift_right)
-        ts(ic(5), ic(5), 5, A.arith_shift_right)
-        ts(it(13, 2), it(13, 2), 3, A.mult)
-        ts(ic(5), ic(5), -3, A.mult)
-        tt(it(13, 2), it(13, 2), it(14, 2), A.add)
-        tt(DEL, ic(5), ic(4), A.add)
-        for i in range(2):
-            ts(w("sd", 2 * i, 2 * i + 2), it(13, 2), fc(20 + i), A.add)
-        ts(w("dm", 0, 24), w("dm", 0, 24), DEL, A.is_equal)
+    def c_last():
+        quant(w("qv", 0, 128), w("svv", 0, 128), w("vt", 0, 512))
+        ts(it(15, 1), it(0, 1), 2, A.is_ge, 20, A.mult)
+        tt(it(15, 1), it(15, 1), it(0, 1), A.add)
+        ts(w("shh", 0, 1), it(15, 1), 23.0, A.min, fc(22), A.add)
 
-    weave(c_spread, c_misc)
+    weave(c_ones, c_ones2)
+    quant(w("qu", 0, 128), w("suu", 0, 128), w("ut", 0, 512))
+    pick(w("qua", 0, 128), w("sua", 0, 128), w("qu", 0, 128), w("suu", 0, 128), LU)
+    turner(0)
+    weave(c_pointers, c_spread)
+    list_u(0, "ext0")
     lists(0, "ext0")
     fan(0)
-    turner(0)
 
     def bwin(b):
         return w("bp", 256 * b, 256 * b + 256)
@@ -430,11 +463,13 @@ def rank_program(g, core, T, topo):
         return w("wq", 128 * b, 128 * b + 128), w("wsc", 128 * b, 128 * b + 128)
 
     def gather(out, b, ind):
-        if b < 2:
+        if b in VG:
             ts(out, bwin(b), 0.015625, A.mult, ind=ind)
         else:
             act(out, bwin(b), scale=0.015625, ind=ind)
 
+    BO = (VG[0], SG[0], VG[1], SG[1])
+    spare += calls(c_seeds) + calls(lambda: turner(1)) + calls(lambda: turner(2)) + calls(c_last)
     for k in range(3):
         h, last = H[k], k == 2
         e = "ext%d" % (k + 1)
@@ -443,156 +478,150 @@ def rank_program(g, core, T, topo):
 
         def unpack_b(b):
             mm(bank(4 + b, 256), *ceb(b), w("bc%d" % k, 0, 256), w("bs%d" % k, 0, 256))
-            if b < 2:
+            if b in VG:
                 copy(bwin(b), bank(4 + b, 256))
             else:
                 act(bwin(b), bank(4 + b, 256))
 
-        def z_of(b):
-            z, gz = w("zt", b, 4 * C, 4), w("gz", C * (b % 2), C * (b % 2) + C)
-            if b < 2:
-                tt(z, bwin(b), fpw(b), A.subtract, ind=lu)
-            else:
-                act(gz, bwin(b), ind=lu)
-                tt(z, gz, bank(b, C), A.subtract)
+        def gz(b):
+            return w("gz", C * b, C * b + C)
 
-        unpack_b(0)
-        z_of(0)
-        unpack_b(2)
-        unpack_b(1)
-        unpack_f(k, (2,))
-        z_of(2)
-        unpack_b(3)
-        unpack_f(k, (3,))
-        z_of(1)
-        z_of(3)
+        for b in SG + VG:
+            unpack_b(b)
+        act(gz(0), bwin(0), ind=lu)
+        if k:
+            for b in VG + SG:
+                mm_f(k, b)
+            copy(fpw(VG[0]), bank(VG[0], C))
+            act(fpw(VG[1]), bank(VG[1], C))
+        act(gz(1), bwin(1), ind=lu)
+        for b in VG:
+            tt(w("zt", b, 4 * C, 4), bwin(b), fpw(b), A.subtract, ind=lu)
+        for b in SG:
+            tt(w("zt", b, 4 * C, 4), gz(b), bank(b, C), A.subtract)
         for t in range(3):
             qz, sz = w("qz", 128 * t, 128 * t + 128), w("sz", 128 * t, 128 * t + 128)
             quant(qz, sz, w("zt", 512 * t, 512 * t + 512))
             mm(bank(4 + t, 128), qz, sz, w("qua", 0, 128), w("sua", 0, 128))
             act(w("sc", 64 * t, 64 * t + 64), bank(4 + t, 128, 64))
         for t in range(3):
-            tt(w("fl", t, 192, 3), bank(4 + t, 64), w("sc", 64 * t, 64 * t + 64), A.is_gt)
-        tt(w("f1", 0, 96), w("fl", 0, 96), w("fl", 96, 192), A.add)
-        tt(w("f2", 0, 96), w("f1", 0, 96), w("sgn", 0, 96), A.mult)
-        tt(w("f3", 0, 48), w("f2", 0, 48), w("f2", 48, 96), A.add)
-        tt(w("rk", 0, 24), w("f3", 0, 24), w("f3", 24, 48), A.add)
-        copy(w("et", 0, 768, 4), w("rk", 0, 32), w("el", 0, 12))
-        act(w("et", 1, 768, 4), w("rk", 0, 32), ind=w("el", 12, 24))
+            p = (64 * t, 64 * t + 64)
+            tt(w("fl", *p), bank(4 + t, 64), w("sc", *p), A.is_gt)
+            scan(w("rk", *p), R1, w("fl", *p))
+        ts(w("et", 0, 768, 4), w("rk", 0, 200), BIG, A.mult, ind=w("el", 0, 12))
+        act(w("et", 1, 768, 4), w("rk", 0, 200), scale=BIG, ind=w("el", 12, 24))
+        idle(1)
         quant(w("qe", 0, 192), w("se", 0, 192), w("et", 0, 768))
         mm(bank(7, 192), w("cc", 128 * k, 128 * k + 128), w("ccs", 128 * k, 128 * k + 128), w("qe", 0, 192), w("se", 0, 192))
-        for b in (2, 3):
+        act(w("lsp", 0, 192), w("lsh", 0, 192), ind=LP, bias=NG)
+        for b in SG:
             act(fpw(b), bank(b, C))
-        tt(w("eq", 0, 192), bank(7, 192), w("gk", 0, 192), A.is_equal)
-        tt(w("pr", 0, 192), w("eq", 0, 192), w("lsh", 0, 192), A.mult)
-        tt(w("p1", 0, 96), w("pr", 0, 96), w("pr", 96, 192), A.add)
-        tt(w("p2", 0, 48), w("p1", 0, 48), w("p1", 48, 96), A.add)
-        tt(w(e, 8, 32), w("p2", 0, 24), w("p2", 24, 48), A.add)
-        halo(k + 1)
-        if last:
+        idle(3)
+        tt(w("un", 0, 192), bank(7, 192), w("lsp", 0, 192), A.add)
+        ts(w("cl2", 0, 192), w("un", 0, 192), 0.0, A.max, 256.0, A.min)
+        scan(w("np", 0, 192), w("r2", 0, 192), w("cl2", 0, 192))
+        ts(w(e, 8, 32), w("np", 7, 192, 8), FX, A.add)
+        halo(k + 1, e)
+        ts(w("exo", 8, 32), w("np", 7, 192, 8), FX, A.add)
+        copy(w("mi", 0, 32), w("exo", 0, 40), sh)
+        a, z = 32 * h, C - 32 * h
+        for b in BO:
+            gather(w("yt", 4 * a + b, 4 * z, 4), b, w("mi", a // 16, z // 16))
+        if not last:
+            qf, sf = w("qf%d" % k, 0, 128), w("sf%d" % k, 0, 128)
+            pick(qf, sf, w("qs%d" % k, 0, 128), w("ss%d" % k, 0, 128), LH)
+            idle(10 if k == 0 else 20)
+            for b in range(4):
+                mm(bank(b, 128), *ceb(b), qf, sf, True, False)
+            tt(w("sm", 0, 32), w(e, 0, 40), w("dm", 0, 32), A.mult, ind=sh)
+            scan(w("s2", 0, 24), R3, w("sm", 0, 24))
+            copy(sv, w("s2", 2, 24, 3))
+            for b in BO:
+                gather(w("ys", b, 512, 4), b, sv)
+            turn(k, H[k + 1] - h, 0, 40)
+            quant(w("qys", 0, 128), w("sys0", 0, 128), w("ys", 0, 512))
+            copy(w("mu", 0, 32), w(e, 0, 40), sh)
+            idle(1)
+            for b in range(4):
+                mm(bank(b, 128), *wb(b), w("qys", 0, 128), w("sys0", 0, 128), False, True)
+            for b in range(4):
+                tt(w("xsd", b, 256, 4), bank(b, 128, 0, 2), w("bp", 256 * b + 64 * rank, 256 * b + 64 * rank + 64), A.max)
+            quant(w("qs%d" % (k + 1), 0, 128), w("ss%d" % (k + 1), 0, 128), w("xsd", 0, 512))
+            seeds(k + 1)
+            for b in BO:
+                gather(w("yt", b, 4 * a, 4), b, w("mu", 0, a // 16))
+                gather(w("yt", 4 * z + b, 4 * C, 4), b, w("mu", z // 16, 24))
+            a, z = 0, C
+            lists(k + 1, "exr")
+        else:
             turn(k, -h, 8, 32)
             for b in range(4):
                 act(w("fh", 64 * b, 64 * b + 32), fpw(b, 0, 32))
                 act(w("fh", 64 * b + 32, 64 * b + 64), fpw(b, 352, 384))
-        if k == 0:
-            fill(w("exo", 0, 48), 0.0)
-            weave(c_seeds)
-            for i in range(1, 4):
-                fill(w("ext%d" % i, 40, 48), 0.0)
-            fill(w("exr", 40, 48), 0.0)
-            for i in (1, 2):
-                ts(w("sh", 2 * i, 2 * i + 2), i2, fc(20 + i), A.add)
-            fill(w("xsd", 256, 512), 0.0)
-        tt(w("exo", 8, 32), w("p2", 0, 24), w("p2", 24, 48), A.add)
-        copy(w("mi", 0, 32), w("exo", 0, 48), sh)
-        a, z = 32 * h, C - 32 * h
-        for b in (0, 2, 1, 3):
-            gather(w("yt", 4 * a + b, 4 * z, 4), b, w("mi", a // 16, z // 16))
-        if k == 0:
-            turner(1)
-        if not last:
-            turn(k, H[k + 1] - h, 0, 40)
-            copy(w("sg", 0, 32), w(e, 0, 48), w("sd", 2 * k, 2 * k + 2))
-            tt(w("sm", 0, 24), w("sg", 0, 24), w("dm", 0, 24), A.mult)
-            tt(w("s1", 0, 8), w("sm", 0, 8), w("sm", 8, 16), A.add)
-            tt(w("s2", 0, 8), w("s1", 0, 8), w("sm", 16, 24), A.add)
-            copy(sv, w("s2", 0, 8))
-            for b in (0, 2, 1, 3):
-                gather(w("ys", b, 512, 4), b, sv)
-            quant(w("qys", 0, 128), w("sys0", 0, 128), w("ys", 0, 512))
             for b in range(4):
-                mm(bank(b, 128), *wb(b), w("qys", 0, 128), w("sys0", 0, 128))
-                act(w("rs", 64 * b, 64 * b + 64), bank(b, 128, 0, 2), F.Relu)
-            copy(w("mu", 0, 32), w(e, 0, 48), sh)
-            for b in range(4):
-                tt(w("xsd", b, 256, 4), w("rs", 64 * b, 64 * b + 64), w("bp", 256 * b + 64 * rank, 256 * b + 64 * rank + 64), A.add)
-            quant(w("qs%d" % (k + 1), 0, 128), w("ss%d" % (k + 1), 0, 128), w("xsd", 0, 512))
-            seeds(k + 1)
-            for b in (0, 2, 1, 3):
-                gather(w("yt", b, 4 * a, 4), b, w("mu", 0, a // 16))
-                gather(w("yt", 4 * z + b, 4 * C, 4), b, w("mu", z // 16, 24))
-            a, z = 0, C
+                mm(bank(b, 128), *ceb(b), w("qf2", 0, 128), w("sf2", 0, 128), True, False)
         xn, n = "xt%d" % (k + 1), z - a
         qy, sy = w("qy", a, z), w("sy", a, z)
         quant(qy, sy, w("yt", 4 * a, 4 * z))
+        if k == 0:
+            idle(1)
         for b in range(4):
             mm(bank(4 + b, n), *ceb(b), w("qx%d" % k, a, z), w("sx%d" % k, a, z), True, False)
         for b in range(4):
             mm(bank(4 + b, n), *wb(b), qy, sy, False, True)
+        if last:
+            copy(w("mh", 0, 16), w(e, 0, 40), w("shh", 0, 1))
+            for b in BO:
+                gather(w("yh", b, 256, 4), b, w("mh", 0, 4))
+        for b in range(4):
             tt(w(xn, 4 * a + b, 4 * z, 4), bank(4 + b, n), fpw(b, a, z), A.max)
-        if not last:
-            lists(k + 1, "exr")
+            if last and b == 1:
+                quant(w("qyh", 0, 128), w("syh", 0, 128), w("yh", 0, 512))
+                for c in range(4):
+                    mm(bank(c, 128), *wb(c), w("qyh", 0, 128), w("syh", 0, 128), False, True)
         quant(w("qx%d" % (k + 1), a, z), w("sx%d" % (k + 1), a, z), w(xn, 4 * a, 4 * z))
         if not last:
-            unpack_f(k + 1, (0, 1))
+            list_u(k + 1, "exr")
             fan(k + 1)
-        if k == 0:
-            fill(w("yh", 256, 512), 0.0)
         if k == 1:
-            quant(w("qv", 0, 128), w("svv", 0, 128), w("vt", 0, 512))
-            ts(it(15, 1), it(0, 1), 2, A.is_ge, 20, A.mult)
-            tt(it(15, 1), it(15, 1), it(0, 1), A.add)
-            ts(w("shh", 0, 1), it(15, 1), fc(22), A.add)
-            turner(2)
+            for p, q, o in ((0, 32, 0), (32, 64, C - 32), (64, 128, 0)):
+                qo, qi, so, si = w("qf2", p, q), w("qx2", o, o + q - p), w("sf2", p, q), w("sx2", o, o + q - p)
+                dma("y", ap(qo).bitcast(dt.uint8), ap(qi).bitcast(dt.uint8), "eg", [qi], [qo])
+                dma("y", ap(so), ap(si), "eg", [si], [so])
 
     qv, svv = w("qv", 0, 128), w("svv", 0, 128)
-    x3, s3 = w("qx3", 32, 352), w("sx3", 32, 352)
-    mm(bank(4, 320), qv, svv, x3, s3)
-    act(w("yo", 32, 352), bank(4, 320))
+    for i, (a, z) in enumerate(((32, 192), (192, 352))):
+        mm(bank(4 + i, z - a), qv, svv, w("qx3", a, z), w("sx3", a, z))
+        act(w("yo", a, z), bank(4 + i, z - a))
 
     def out_scales(c0, c1, name, a, b):
         for i in range(4):
             dma("y", T.osc[4 * i:4 * i + 4, c0:c1], ap(w(name, a, b, 1, 32 * i, 32 * i + 4)), "st", [w(name, a, b)], [])
 
-    copy(w("mh", 0, 16), w("ext3", 0, 48), w("shh", 0, 1))
-    for b in (0, 2, 1, 3):
-        gather(w("yh", b, 256, 4), b, w("mh", 0, 4))
-    quant(w("qys", 0, 128), w("sys0", 0, 128), w("yh", 0, 512))
     for b in range(4):
-        mm(bank(b, 128), *wb(b), w("qys", 0, 128), w("sys0", 0, 128))
-        act(w("rs", 64 * b, 64 * b + 64), bank(b, 64), F.Relu)
-    for b in range(4):
-        tt(w("xsd", b, 256, 4), w("rs", 64 * b, 64 * b + 64), w("fh", 64 * b, 64 * b + 64), A.add)
-    quant(w("qh", 0, 128), w("sh0", 0, 128), w("xsd", 0, 512))
+        tt(w("xhd", b, 256, 4), bank(b, 64), w("fh", 64 * b, 64 * b + 64), A.max)
+    quant(w("qh", 0, 128), w("sh0", 0, 128), w("xhd", 0, 512))
     mm(bank(7, 128), qv, svv, w("qh", 0, 128), w("sh0", 0, 128))
     act(w("yo2", 0, 64), bank(7, 64))
-    pn = w("pi", 0, 24)
-    fill(w("on", 24, 32), 0.0)
+    pn = w("po", 0, 24)
     copy(pn, w("exr", 8, 32))
+    fill(w("on", 24, 32), 0.0)
     relabel(w("on", 0, 24), pn, 24)
     op("v", lambda: vec.transpose(ap(w("ot", 0, 32)), ap(w("on", 0, 32))), [w("on", 0, 32)], [w("ot", 0, 32)])
-    dma("y", T.oc[:, 128:1408], ap(x3).bitcast(dt.uint8), "st", [x3], [])
+    dma("y", T.oc[:, 128:1408], ap(w("qx3", 32, 352)).bitcast(dt.uint8), "st", [w("qx3", 32, 352)], [])
     out_scales(32, 352, "sx3", 32, 352)
-    dma("y", T.y[:, 32:352], ap(w("yo", 32, 352)), "st", [w("yo", 32, 352)], [])
+    for a, z in ((32, 192), (192, 352)):
+        dma("y", T.y[:, a:z], ap(w("yo", a, z)), "st", [w("yo", a, z)], [])
     for a, b in ((0, 0), (32, 352)):
         v = w("qh", a, a + 32)
         dma("y", T.oc[:, 4 * b:4 * b + 128], ap(v).bitcast(dt.uint8), "st", [v], [])
         out_scales(b, b + 32, "sh0", a, a + 32)
+    for a, b in ((0, 0), (32, 352)):
         v = w("yo2", a, a + 32)
         dma("s", T.y[:, b:b + 32], ap(v), "st", [v], [])
     for m in range(8):
         v = w("ot", 16 * (m % 2), 16 * (m % 2) + 16, 1, 32 * (m // 2), 32 * (m // 2) + 24)
-        dma("y", T.op[m:m + 1, :], ap(v), "st", [v], [])
+        dma("s", T.op[m:m + 1, :], ap(v), "st", [v], [])
     for sem in SEMAPHORES:
         if total.get(sem, 0):
             wait("g", sem, total[sem])

from concourse.bass import DstId, RemoteDMATransfer
from concourse.mybir import dt, AluOpType, ActivationFunctionType

C = 384
H = [4, 2, 1]
DC = [0, 1, 1, 1, 0, -1, -1, -1]
SG, VG = (0, 1), (2, 3)
BIG = 512.0

SCRATCH = {}


def _b(name, cols, dtype, where="sbuf"):
    SCRATCH[name] = (where, [128, cols], dtype)


X4, U8, BF, F32, I32, U16 = "float8_e4m3fn_x4", "uint8", "bfloat16", "float32", "int32", "uint16"
for _i in range(8):
    _b("ps%d" % _i, 512, F32, "psum")
for _r in range(4):
    _b("xt%d" % _r, 4 * C, BF)
    _b("qx%d" % _r, C, X4)
    _b("sx%d" % _r, C, U8)
    _b("ext%d" % _r, 40, F32)
for _r in range(3):
    _b("bc%d" % _r, 256, X4)
    _b("bs%d" % _r, 256, U8)
    _b("qs%d" % _r, 128, X4)
    _b("ss%d" % _r, 128, U8)
    _b("qf%d" % _r, 128, X4)
    _b("sf%d" % _r, 128, U8)
    SCRATCH["fan%d" % _r] = ("dram", [48, 8, 24], F32)
for _n, _c, _t in (("fp", 4 * C, BF), ("bp", 1024, BF), ("gz", 2 * C, BF), ("zt", 4 * C, BF), ("yt", 4 * C, BF), ("ys", 512, BF), ("yh", 512, BF), ("xsd", 512, BF), ("xhd", 512, BF), ("fh", 256, BF),
                   ("exs", 40, F32), ("exr", 40, F32), ("lf", 32, F32), ("lw", 24, F32), ("lu", 32, U16), ("mi", 32, U16), ("mu", 32, U16), ("sv", 8, U16), ("lsh", 192, F32), ("lsp", 192, F32),
                   ("qz", C, X4), ("sz", C, U8), ("qy", C, X4), ("sy", C, U8), ("qys", 128, X4), ("sys0", 128, U8), ("qyh", 128, X4), ("syh", 128, U8), ("qh", 128, X4), ("sh0", 128, U8),
                   ("sc", 192, F32), ("fl", 192, F32), ("rr", 88, F32), ("rk", 200, F32), ("exo", 40, F32),
                   ("et", 768, BF), ("qe", 192, X4), ("se", 192, U8), ("un", 192, BF), ("cl2", 192, BF), ("r2", 192, BF), ("np", 192, F32),
                   ("sm", 32, F32), ("s2", 24, F32), ("yo", C, F32), ("yo2", 64, F32), ("mh", 16, U16),
                   ("ut", 512, BF), ("vt", 512, BF), ("qu", 128, X4), ("suu", 128, U8), ("qua", 128, X4), ("sua", 128, U8), ("qv", 128, X4), ("svv", 128, U8),
                   ("wq", 512, X4), ("wsc", 512, U8), ("one", 528, BF), ("wd", 528, BF), ("ce", 512, X4), ("cs", 512, U8), ("ct", 1536, BF), ("cc", 384, X4), ("ccs", 384, U8),
                   ("pi", 40, I32), ("po", 24, I32), ("kk", 160, I32), ("pf", 40, F32), ("pd", 20, F32), ("pe", 20, F32),
                   ("ip", 16, I32), ("i12", 12, I32), ("cl", 32, F32), ("it", 240, I32), ("ul", 20, U16), ("sh", 6, U16), ("shh", 2, U16), ("el", 36, U16),
                   ("q0", 128, F32), ("dm", 33, F32), ("on", 32, F32), ("ot", 32, F32)):
    _b(_n, _c, _t)
SEMAPHORES = ["kv", "ks", "kt", "kg", "lx", "lp", "lu", "lw", "lv", "st", "eg", "loc", "ha0", "ha1", "ha2", "ha3"]
for _r in range(3):
    SEMAPHORES += ["se%d" % _r, "ow%d" % _r, "rr%d" % _r, "fw%d" % _r, "fr%d" % _r]


def rank_program(g, core, T, topo):
    rank = T.rank_of(core)
    if rank is None:
        return
    A, F = AluOpType, ActivationFunctionType
    N = len(T.cores)
    vec, sca, ten, syn = g.vector, g.scalar, g.tensor, g.sync
    queue = {"v": vec, "s": sca, "t": ten, "g": g, "y": syn}
    total, seen, log, hold = {}, {q: {} for q in queue}, {}, []

    def w(name, a, b, step=1, p0=0, p1=128):
        return (name, a, b, step, p0, p1)

    def ap(v):
        name, a, b, step, p0, p1 = v
        t = T[name]
        if p0 == 0 and p1 == 128:
            return t[:, a:b] if step == 1 else t[:, a:b:step]
        return t[p0:p1, a:b] if step == 1 else t[p0:p1, a:b:step]

    def meet(x, y):
        if x[1] >= y[2] or y[1] >= x[2] or x[4] >= y[5] or y[4] >= x[5]:
            return False
        return not (x[3] == y[3] and x[3] > 1 and (x[1] - y[1]) % x[3])

    def wait(q, sem, val):
        if seen[q].get(sem, 0) < val:
            queue[q].wait_ge(T.sem[sem], int(val))
            seen[q][sem] = val

    def order(q, reads, writes, acc, dma):
        for vs, wr in ((reads, False), (writes, True)):
            for v in vs:
                bank = v[0][:2] == "ps"
                for (o, owr, oq, osem, oval, odma) in log.get(v[0], ()):
                    if not (bank or meet(v, o)):
                        continue
                    if not (wr or owr or (bank and oq != q)):
                        continue
                    if oq == q and not odma and not dma:
                        if (acc and wr) or not owr:
                            continue
                    wait(q, osem, total[osem] if odma else oval)

    def note(q, reads, writes, sem, val, dma):
        for v in writes:
            old = log.get(v[0], [])
            log[v[0]] = [e for e in old if not (v[3] == 1 and v[1] <= e[0][1] and v[2] >= e[0][2] and v[4] <= e[0][4] and v[5] >= e[0][5])]
            log[v[0]].append((v, True, q, sem, val, dma))
        for v in reads:
            log.setdefault(v[0], []).append((v, False, q, sem, val, dma))

    def op(q, call, reads, writes, acc=False):
        if hold:
            hold[-1].append((q, call, reads, writes, acc))
            return
        order(q, reads, writes, acc, False)
        sem = "k" + q
        total[sem] = total.get(sem, 0) + 1
        call().then_inc(T.sem[sem], 1)
        note(q, reads, writes, sem, total[sem], False)

    def calls(c):
        hold.append([])
        c()
        return hold.pop()

    def weave(*chains):
        lists = [calls(c) for c in chains]
        for i in range(max(len(x) for x in lists)):
            for x in lists:
                if i < len(x):
                    op(*x[i])

    spare = []

    def idle(n):
        for _ in range(min(n, len(spare))):
            op(*spare.pop(0))

    def dma(q, out, in_, sem, reads, writes, after=()):
        order(q, reads, writes, False, True)
        for s in after:
            wait(q, s, total[s])
        total[sem] = total.get(sem, 0) + 16
        queue[q].dma_start(out, in_).then_inc(T.sem[sem], 16)
        note(q, reads, writes, sem, total[sem], True)

    def arrive(v, sem, val):
        total[sem] = val
        log.setdefault(v[0], []).append((v, True, "r", sem, val, True))

    def at(v, ind):
        return ap(v) if ind is None else ap(v).indirect(ap(ind))

    def rd(v, ind):
        return [v] if ind is None else [v, ind]

    def copy(out, in_, ind=None):
        op("v", lambda: vec.tensor_copy(ap(out), at(in_, ind)), rd(in_, ind), [out])

    def tt(out, a, b, o, ind=None):
        op("v", lambda: vec.tensor_tensor(ap(out), at(a, ind), ap(b), o), rd(a, ind) + [b], [out])

    def ts(out, a, s1, o1, s2=None, o2=None, ind=None):
        more = [s for s in (s1, s2) if isinstance(s, tuple)]
        n1, n2 = [ap(s) if isinstance(s, tuple) else s for s in (s1, s2)]
        if o2 is None:
            op("v", lambda: vec.tensor_scalar(ap(out), at(a, ind), n1, None, o1), rd(a, ind) + more, [out])
        else:
            op("v", lambda: vec.tensor_scalar(ap(out), at(a, ind), n1, n2, o1, o2), rd(a, ind) + more, [out])

    def scan(out, d0, d1):
        op("v", lambda: vec.tensor_tensor_scan(ap(out), ap(d0), ap(d1), 0.0, A.mult, A.add), [d0, d1], [out])

    def fill(out, val):
        op("v", lambda: vec.memset(ap(out), val), [], [out])

    def act(out, in_, scale=1.0, ind=None, bias=None):
        if bias is not None:
            op("s", lambda: sca.activation(ap(out), at(in_, ind), F.Identity, bias=ap(bias)), rd(in_, ind) + [bias], [out])
        elif scale == 1.0:
            op("s", lambda: sca.activation(ap(out), at(in_, ind), F.Copy), rd(in_, ind), [out])
        else:
            op("s", lambda: sca.activation(ap(out), at(in_, ind), F.Copy, scale=scale), rd(in_, ind), [out])

    def quant(q, s, in_):
        op("v", lambda: vec.quantize_mx(ap(q), ap(s), ap(in_)), [in_], [q, s])

    def mm(out, l, ls, r, rs, start=True, stop=True):
        op("t", lambda: ten.matmul_mx(ap(out), ap(l), ap(ls), ap(r), ap(rs), start, stop), [l, ls, r, rs], [out], acc=not start)

    def iota(out, pat, base, cm):
        if SCRATCH[out[0]][2] != I32:
            op("g", lambda: g.iota(ap(out), pat, base, cm, allow_small_or_imprecise_dtypes=True), [], [out])
        else:
            op("g", lambda: g.iota(ap(out), pat, base, cm), [], [out])

    def pick(qo, so, qi, si, ind):
        op("v", lambda: vec.tensor_copy(ap(qo).bitcast(dt.uint32), ap(qi).bitcast(dt.uint32).indirect(ap(ind))), [qi, ind], [qo])
        act(so, si, ind=ind)

    up, down = (rank - 1) % N, (rank + 1) % N
    others = [r for r in range(N) if r != rank]

    def dst(r):
        rid, pid, _ = topo.addr(T.cores[r])
        return DstId(rid=rid, pnc=pid)

    def bits(es):
        return sum(1 << e for e in es)

    def fused(trs, reads):
        order("g", reads, [], False, True)
        total["loc"] = total.get("loc", 0) + sum(bin(m).count("1") for _, m, _, _, _ in trs)
        g.remote_dma_fused([RemoteDMATransfer(dst_ids=ids, dma_engine_mask=m, remote_sem=T.sem[sem], srcs=[src], dsts=dsts) for ids, m, sem, src, dsts in trs], local_sem=T.sem["loc"])

    def halo(k, e):
        s = "ha%d" % k
        eu, ed = topo.engines(core, T.cores[up]), topo.engines(core, T.cores[down])
        hu, hd = eu[:len(eu) // 2], ed[len(ed) // 2:]
        lo, hi = w(e, 8, 16), w(e, 24, 32)
        fused([([dst(up)], bits(hu), s, ap(lo), [ap(w(e, 32, 40))]), ([dst(down)], bits(hd), s, ap(hi), [ap(w(e, 0, 8))])], [lo, hi])
        arrive(w(e, 0, 8), s, len(hu) + len(hd))
        arrive(w(e, 32, 40), s, len(hu) + len(hd))

    def seeds(k):
        m = bits(topo.engines(core, T.cores[others[0]]))
        ids = [dst(r) for r in others]
        a, b = 64 * rank, 64 * rank + 64
        q, s, bq, bs = w("qs%d" % k, 0, 64), w("ss%d" % k, 0, 64), w("bc%d" % k, a, b), w("bs%d" % k, a, b)
        fused([(ids, m, "se%d" % k, ap(q).bitcast(dt.uint8), [ap(bq).bitcast(dt.uint8) for r in others])], [q])
        fused([(ids, m, "se%d" % k, ap(s), [ap(bs) for r in others])], [s])
        dma("y", ap(bq).bitcast(dt.uint8), ap(q).bitcast(dt.uint8), "ow%d" % k, [q], [bq])
        dma("y", ap(bs), ap(s), "ow%d" % k, [s], [bs])
        n = 2 * len(others) * bin(m).count("1")
        for r in others:
            arrive(w("bc%d" % k, 64 * r, 64 * r + 64), "se%d" % k, n)
            arrive(w("bs%d" % k, 64 * r, 64 * r + 64), "se%d" % k, n)

    def turned(s):
        for m in range(8):
            d = s * DC[m]
            if d == 0:
                yield m, 0, 16, 0, False
            elif d > 0:
                yield m, 0, 16 - d, d, False
                yield m, 16 - d, 16, 0, True
            else:
                yield m, -d, 16, 0, False
                yield m, 0, -d, 16 + d, True

    for m, a, b, o, _ in turned(H[0]):
        v = w("pi", 8, 32, 1, 16 * m + a, 16 * m + b)
        dma("s", ap(v), T.p[16 * m + o:16 * m + o + b - a, :], "lp", [], [v])
    dma("y", ap(w("xt0", 0, 4 * C)), T.x[:, :], "lx", [], [w("xt0", 0, 4 * C)])
    dma("y", ap(w("ut", 0, 512)), T.u[:, :], "lu", [], [w("ut", 0, 512)])
    dma("y", ap(w("wq", 0, 512)).bitcast(dt.uint8), T.wc[:, :], "lw", [], [w("wq", 0, 512)])
    dma("y", ap(w("wsc", 0, 512)), T.ws[:, :], "lw", [], [w("wsc", 0, 512)])
    dma("y", ap(w("vt", 0, 512)), T.v[:, :], "lv", [], [w("vt", 0, 512)])

    def ic(i):
        return w("ip", i, i + 1)

    def fc(i):
        return w("cl", i, i + 1)

    def it(i, n):
        return w("it", 12 * i, 12 * i + n)

    P, GI, QI = ic(0), ic(1), ic(2)
    GF, QF, G16, DR1, CAR, DEL, GX = [fc(i) for i in range(7)]
    MG, NG, FX = fc(24), fc(25), fc(26)
    idx, i8, i4, i2 = it(0, 12), it(0, 8), it(0, 4), it(0, 2)
    LU, LH, LS, LP = w("ul", 0, 8), w("ul", 8, 16), w("ul", 16, 20), w("el", 24, 36)
    R1, R3 = w("rr", 0, 64), w("rr", 64, 88)

    fill(w("one", 0, 515), 1.0)
    iota(P, [[0, 1]], 0, 1)
    iota(w("i12", 0, 12), [[16, 12]], 0, 1)
    op("g", lambda: g.affine_select(ap(w("wd", 0, 515)), ap(w("one", 0, 515)), [[-1, 515]], A.is_equal, 0.0, 3, 4), [w("one", 0, 515)], [w("wd", 0, 515)])
    iota(w("q0", 0, 128), [[0, 8], [1, 16]], 0, 0)
    halo(0, "pi")

    def zeros(v):
        act(v, w("one", 0, v[2] - v[1]), scale=0.0)

    for v in (w("ct", 0, 512), w("exo", 0, 40), w("xsd", 256, 512), w("yh", 256, 512), w("xhd", 256, 512)):
        zeros(v)

    ts(GI, P, 4, A.arith_shift_right)
    ts(QI, P, 15, A.bitwise_and)
    copy(GF, GI)
    copy(QF, QI)
    ts(G16, GF, -16.0, A.mult)
    ts(idx, w("i12", 0, 12), G16, A.add)

    def relabel(out, p, n):
        k = [w("kk", 40 * i, 40 * i + n) for i in range(4)]
        ts(k[0], p, 7, A.bitwise_and)
        ts(k[1], k[0], 3, A.mult)
        ts(k[2], k[1], 7, A.bitwise_and)
        tt(k[3], k[2], k[0], A.subtract)
        tt(out, k[3], p, A.add)

    def c_own():
        relabel(it(17, 4), i4, 4)
        ts(LS, it(17, 4), 6.0, A.mult)

    def c_rows():
        ts(fc(8), GF, 2.0, A.is_ge)
        ts(fc(9), GF, 3.0, A.is_ge, fc(8), A.add)
        tt(DR1, fc(9), fc(11), A.subtract)
        for i, h in enumerate(H):
            ts(fc(20 + i), DR1, 2.0 * h, A.mult, 8.0 - 2.0 * h, A.add)
        for i in range(3):
            ts(w("sh", 2 * i, 2 * i + 2), i2, 23.0, A.min, fc(20 + i), A.add)

    def c_rows2():
        ts(fc(10), GF, 6.0, A.is_ge)
        ts(fc(11), GF, 7.0, A.is_ge, fc(10), A.add)
        ts(it(18, 8), i8, 1, A.arith_shift_right)
        ts(LH, it(18, 8), 0, A.add)

    def c_carry():
        ts(fc(12), GF, 4.0, A.is_ge)
        ts(fc(13), GF, 1.0, A.is_ge, fc(12), A.subtract)
        ts(fc(15), GF, 5.0, A.is_ge)
        ts(fc(14), QF, float(16 - H[0]), A.is_ge, fc(13), A.mult)
        ts(fc(16), QF, float(H[0]), A.is_lt, fc(15), A.mult)
        tt(CAR, fc(14), fc(16), A.add)

    def c_pairs():
        ts(it(1, 4), i4, 3, A.arith_shift_right)
        ts(it(3, 4), i4, 7, A.bitwise_and)
        tt(it(4, 4), it(1, 4), it(3, 4), A.max)
        tt(w("it", 52, 56), it(1, 4), it(3, 4), A.min)
        ts(LU, it(4, 8), 16, A.mult)

    def c_half():
        ts(ic(3), GI, 1, A.bitwise_and)
        ts(fc(7), ic(3), -2.0, A.mult, 1.0, A.add)
        tt(GX, fc(7), GF, A.add)
        ts(MG, GF, BIG, A.mult)
        ts(NG, GF, -BIG, A.mult)
        ts(FX, GF, 256.0, A.mult, -7.0 * 256.0, A.add)

    def c_ones():
        fill(R1, 1.0)
        ts(w("rr", 0, 64, 8), w("rr", 0, 64, 8), 0.0, A.mult)
        ts(w("rr", 9, 64, 9), w("rr", 9, 64, 9), -1.0, A.mult)
        fill(w("rk", 192, 200), 0.0)

    def c_ones2():
        fill(w("r2", 0, 192), 1.0)
        ts(w("r2", 0, 192, 8), w("r2", 0, 192, 8), 0.0, A.mult)
        fill(R3, 1.0)
        ts(w("rr", 64, 88, 3), w("rr", 64, 88, 3), 0.0, A.mult)

    weave(c_rows2, c_own, c_pairs)
    weave(c_rows, c_carry, c_half)

    quant(w("qx0", 0, C), w("sx0", 0, C), w("xt0", 0, 4 * C))
    pick(w("qs0", 0, 64), w("ss0", 0, 64), w("qx0", 0, C), w("sx0", 0, C), LS)
    seeds(0)
    iota(w("dm", 0, 33), [[0, 11], [1, 3]], 0, 0)
    iota(w("et", 0, 768), [[0, 768]], 0, 0)
    iota(w("ct", 512, 1536), [[0, 1024]], 0, 0)
    for b in VG + SG:
        quant(w("ce", 128 * b, 128 * b + 128), w("cs", 128 * b, 128 * b + 128), w("wd", 3 - b, 515 - b))

    def bank(b, n, a=0, step=1):
        return w("ps%d" % b, a, n, step)

    def ceb(b):
        return w("ce", 128 * b, 128 * b + 128), w("cs", 128 * b, 128 * b + 128)

    def fpw(b, a=0, e=C):
        return w("fp", C * b + a, C * b + e)

    def mm_f(k, b):
        mm(bank(b, C), *ceb(b), w("qx%d" % k, 0, C), w("sx%d" % k, 0, C))

    for b in VG + SG:
        mm_f(0, b)
    for b in VG:
        act(fpw(b), bank(b, C))

    def c_pointers():
        relabel(w("pf", 0, 40), w("pi", 0, 40), 40)
        tt(w("pd", 0, 20), w("pf", 1, 40, 2), w("pf", 0, 40, 2), A.subtract)
        ts(w("pe", 0, 20), w("pd", 0, 20), CAR, A.mult)
        tt(w("ext0", 0, 40, 2), w("pf", 0, 40, 2), w("pe", 0, 20), A.add)
        tt(w("ext0", 1, 40, 2), w("pf", 1, 40, 2), w("pe", 0, 20), A.subtract)

    def lists(k, src):
        act(w("lf", 0, 32), w(src, 0, 40), ind=w("sh", 2 * k, 2 * k + 2), bias=MG)

    def list_u(k, src):
        copy(w("lu", 0, 32), w(src, 0, 40), w("sh", 2 * k, 2 * k + 2))

    def fan(k):
        t = T["fan%d" % k]
        act(w("lw", 0, 24, 2), w("lf", 1, 24, 2))
        act(w("lw", 1, 24, 2), w("lf", 0, 24, 2))
        for j, n in ((1, "lf"), (0, "lw"), (2, "lw")):
            for m in range(8):
                v = w(n, 0, 24, 1, 16 * m, 16 * m + 16)
                dma("y", t[16 * j:16 * j + 16, m, :], ap(v), "fw%d" % k, [v], [])
        for m in range(8):
            o = w("lsh", 0, 192, 1, 16 * m, 16 * m + 16)
            a = 16 + H[k] * DC[m]
            dma("y", ap(o), t[a:a + 16, :, :], "fr%d" % k, [], [o], ["fw%d" % k])

    def turn(k, s, a, b):
        e = "ext%d" % (k + 1)
        act(w("exs", a, b, 2), w(e, a + 1, b, 2))
        act(w("exs", a + 1, b, 2), w(e, a, b, 2))
        for m, p, q, o, swap in sorted(turned(s), key=lambda x: x[4]):
            v, d = w("exs" if swap else e, a, b, 1, 16 * m + o, 16 * m + o + q - p), w("exr", a, b, 1, 16 * m + p, 16 * m + q)
            dma("y", ap(d), ap(v), "rr%d" % k, [v], [d])

    def c_spread():
        n = [it(i, 12) for i in range(6, 13)]
        ts(n[0], idx, 7, A.bitwise_and)
        ts(n[1], idx, 3, A.arith_shift_right)
        ts(n[2], n[1], 24, A.bitwise_and)
        ts(n[3], n[1], 7, A.bitwise_and)
        tt(n[4], n[0], n[2], A.add)
        ts(n[4], n[4], 8, A.mult, 7 - 192, A.add)
        ts(n[5], n[3], GF, A.is_equal)
        ts(n[6], n[3], GX, A.is_equal)
        tt(n[5], n[5], n[4], A.mult)
        tt(n[6], n[6], n[4], A.mult)
        ts(w("el", 0, 12), n[5], 192, A.add)
        ts(w("el", 12, 24), n[6], 192, A.add)
        ts(n[2], n[0], 24, A.mult)
        tt(n[2], n[2], n[1], A.add)
        ts(LP, n[2], 0, A.add)

    def c_seeds():
        ts(ic(4), QI, 1, A.arith_shift_right)
        ts(ic(5), ic(4), 11, A.mult)
        ts(ic(5), ic(5), 5, A.arith_shift_right)
        ts(ic(5), ic(5), -3, A.mult)
        tt(DEL, ic(5), ic(4), A.add)
        ts(w("dm", 0, 33), w("dm", 0, 33), DEL, A.is_equal)

    def turner(i):
        h = H[i]
        for (g0, g1, d, e) in ((0, 1, 0, 0), (1, 4, h, 0), (1, 4, h - 16, 1), (4, 5, 0, 0), (5, 8, -h, 0), (5, 8, 16 - h, 1)):
            ts(w("ct", 512 * i + 64 * g0 + e, 512 * i + 64 * g1, 4), w("q0", 16 * g0, 16 * g1), float(d), A.add, QF, A.is_equal)
        quant(w("cc", 128 * i, 128 * i + 128), w("ccs", 128 * i, 128 * i + 128), w("ct", 512 * i, 512 * i + 512))

    def c_last():
        quant(w("qv", 0, 128), w("svv", 0, 128), w("vt", 0, 512))
        ts(it(15, 1), it(0, 1), 2, A.is_ge, 20, A.mult)
        tt(it(15, 1), it(15, 1), it(0, 1), A.add)
        ts(w("shh", 0, 1), it(15, 1), 23.0, A.min, fc(22), A.add)

    weave(c_ones, c_ones2)
    quant(w("qu", 0, 128), w("suu", 0, 128), w("ut", 0, 512))
    pick(w("qua", 0, 128), w("sua", 0, 128), w("qu", 0, 128), w("suu", 0, 128), LU)
    turner(0)
    weave(c_pointers, c_spread)
    list_u(0, "ext0")
    lists(0, "ext0")
    fan(0)

    def bwin(b):
        return w("bp", 256 * b, 256 * b + 256)

    def wb(b):
        return w("wq", 128 * b, 128 * b + 128), w("wsc", 128 * b, 128 * b + 128)

    def gather(out, b, ind):
        if b in VG:
            ts(out, bwin(b), 0.015625, A.mult, ind=ind)
        else:
            act(out, bwin(b), scale=0.015625, ind=ind)

    BO = (VG[0], SG[0], VG[1], SG[1])
    spare += calls(c_seeds) + calls(lambda: turner(1)) + calls(lambda: turner(2)) + calls(c_last)
    for k in range(3):
        h, last = H[k], k == 2
        e = "ext%d" % (k + 1)
        lu, sv = w("lu", 0, 24), w("sv", 0, 8)
        sh = w("sh", 2 * k, 2 * k + 2)

        def unpack_b(b):
            mm(bank(4 + b, 256), *ceb(b), w("bc%d" % k, 0, 256), w("bs%d" % k, 0, 256))
            if b in VG:
                copy(bwin(b), bank(4 + b, 256))
            else:
                act(bwin(b), bank(4 + b, 256))

        def gz(b):
            return w("gz", C * b, C * b + C)

        for b in SG + VG:
            unpack_b(b)
        act(gz(0), bwin(0), ind=lu)
        if k:
            for b in VG + SG:
                mm_f(k, b)
            copy(fpw(VG[0]), bank(VG[0], C))
            act(fpw(VG[1]), bank(VG[1], C))
        act(gz(1), bwin(1), ind=lu)
        for b in VG:
            tt(w("zt", b, 4 * C, 4), bwin(b), fpw(b), A.subtract, ind=lu)
        for b in SG:
            tt(w("zt", b, 4 * C, 4), gz(b), bank(b, C), A.subtract)
        for t in range(3):
            qz, sz = w("qz", 128 * t, 128 * t + 128), w("sz", 128 * t, 128 * t + 128)
            quant(qz, sz, w("zt", 512 * t, 512 * t + 512))
            mm(bank(4 + t, 128), qz, sz, w("qua", 0, 128), w("sua", 0, 128))
            act(w("sc", 64 * t, 64 * t + 64), bank(4 + t, 128, 64))
        for t in range(3):
            p = (64 * t, 64 * t + 64)
            tt(w("fl", *p), bank(4 + t, 64), w("sc", *p), A.is_gt)
            scan(w("rk", *p), R1, w("fl", *p))
        ts(w("et", 0, 768, 4), w("rk", 0, 200), BIG, A.mult, ind=w("el", 0, 12))
        act(w("et", 1, 768, 4), w("rk", 0, 200), scale=BIG, ind=w("el", 12, 24))
        idle(1)
        quant(w("qe", 0, 192), w("se", 0, 192), w("et", 0, 768))
        mm(bank(7, 192), w("cc", 128 * k, 128 * k + 128), w("ccs", 128 * k, 128 * k + 128), w("qe", 0, 192), w("se", 0, 192))
        act(w("lsp", 0, 192), w("lsh", 0, 192), ind=LP, bias=NG)
        for b in SG:
            act(fpw(b), bank(b, C))
        idle(3)
        tt(w("un", 0, 192), bank(7, 192), w("lsp", 0, 192), A.add)
        ts(w("cl2", 0, 192), w("un", 0, 192), 0.0, A.max, 256.0, A.min)
        scan(w("np", 0, 192), w("r2", 0, 192), w("cl2", 0, 192))
        ts(w(e, 8, 32), w("np", 7, 192, 8), FX, A.add)
        halo(k + 1, e)
        ts(w("exo", 8, 32), w("np", 7, 192, 8), FX, A.add)
        copy(w("mi", 0, 32), w("exo", 0, 40), sh)
        a, z = 32 * h, C - 32 * h
        for b in BO:
            gather(w("yt", 4 * a + b, 4 * z, 4), b, w("mi", a // 16, z // 16))
        if not last:
            qf, sf = w("qf%d" % k, 0, 128), w("sf%d" % k, 0, 128)
            pick(qf, sf, w("qs%d" % k, 0, 128), w("ss%d" % k, 0, 128), LH)
            idle(10 if k == 0 else 20)
            for b in range(4):
                mm(bank(b, 128), *ceb(b), qf, sf, True, False)
            tt(w("sm", 0, 32), w(e, 0, 40), w("dm", 0, 32), A.mult, ind=sh)
            scan(w("s2", 0, 24), R3, w("sm", 0, 24))
            copy(sv, w("s2", 2, 24, 3))
            for b in BO:
                gather(w("ys", b, 512, 4), b, sv)
            turn(k, H[k + 1] - h, 0, 40)
            quant(w("qys", 0, 128), w("sys0", 0, 128), w("ys", 0, 512))
            copy(w("mu", 0, 32), w(e, 0, 40), sh)
            idle(1)
            for b in range(4):
                mm(bank(b, 128), *wb(b), w("qys", 0, 128), w("sys0", 0, 128), False, True)
            for b in range(4):
                tt(w("xsd", b, 256, 4), bank(b, 128, 0, 2), w("bp", 256 * b + 64 * rank, 256 * b + 64 * rank + 64), A.max)
            quant(w("qs%d" % (k + 1), 0, 128), w("ss%d" % (k + 1), 0, 128), w("xsd", 0, 512))
            seeds(k + 1)
            for b in BO:
                gather(w("yt", b, 4 * a, 4), b, w("mu", 0, a // 16))
                gather(w("yt", 4 * z + b, 4 * C, 4), b, w("mu", z // 16, 24))
            a, z = 0, C
            lists(k + 1, "exr")
        else:
            turn(k, -h, 8, 32)
            for b in range(4):
                act(w("fh", 64 * b, 64 * b + 32), fpw(b, 0, 32))
                act(w("fh", 64 * b + 32, 64 * b + 64), fpw(b, 352, 384))
            for b in range(4):
                mm(bank(b, 128), *ceb(b), w("qf2", 0, 128), w("sf2", 0, 128), True, False)
        xn, n = "xt%d" % (k + 1), z - a
        qy, sy = w("qy", a, z), w("sy", a, z)
        quant(qy, sy, w("yt", 4 * a, 4 * z))
        if k == 0:
            idle(1)
        for b in range(4):
            mm(bank(4 + b, n), *ceb(b), w("qx%d" % k, a, z), w("sx%d" % k, a, z), True, False)
        for b in range(4):
            mm(bank(4 + b, n), *wb(b), qy, sy, False, True)
        if last:
            copy(w("mh", 0, 16), w(e, 0, 40), w("shh", 0, 1))
            for b in BO:
                gather(w("yh", b, 256, 4), b, w("mh", 0, 4))
        for b in range(4):
            tt(w(xn, 4 * a + b, 4 * z, 4), bank(4 + b, n), fpw(b, a, z), A.max)
            if last and b == 1:
                quant(w("qyh", 0, 128), w("syh", 0, 128), w("yh", 0, 512))
                for c in range(4):
                    mm(bank(c, 128), *wb(c), w("qyh", 0, 128), w("syh", 0, 128), False, True)
        quant(w("qx%d" % (k + 1), a, z), w("sx%d" % (k + 1), a, z), w(xn, 4 * a, 4 * z))
        if not last:
            list_u(k + 1, "exr")
            fan(k + 1)
        if k == 1:
            for p, q, o in ((0, 32, 0), (32, 64, C - 32), (64, 128, 0)):
                qo, qi, so, si = w("qf2", p, q), w("qx2", o, o + q - p), w("sf2", p, q), w("sx2", o, o + q - p)
                dma("y", ap(qo).bitcast(dt.uint8), ap(qi).bitcast(dt.uint8), "eg", [qi], [qo])
                dma("y", ap(so), ap(si), "eg", [si], [so])

    qv, svv = w("qv", 0, 128), w("svv", 0, 128)
    for i, (a, z) in enumerate(((32, 192), (192, 352))):
        mm(bank(4 + i, z - a), qv, svv, w("qx3", a, z), w("sx3", a, z))
        act(w("yo", a, z), bank(4 + i, z - a))

    def out_scales(c0, c1, name, a, b):
        for i in range(4):
            dma("y", T.osc[4 * i:4 * i + 4, c0:c1], ap(w(name, a, b, 1, 32 * i, 32 * i + 4)), "st", [w(name, a, b)], [])

    for b in range(4):
        tt(w("xhd", b, 256, 4), bank(b, 64), w("fh", 64 * b, 64 * b + 64), A.max)
    quant(w("qh", 0, 128), w("sh0", 0, 128), w("xhd", 0, 512))
    mm(bank(7, 128), qv, svv, w("qh", 0, 128), w("sh0", 0, 128))
    act(w("yo2", 0, 64), bank(7, 64))
    pn = w("po", 0, 24)
    copy(pn, w("exr", 8, 32))
    fill(w("on", 24, 32), 0.0)
    relabel(w("on", 0, 24), pn, 24)
    op("v", lambda: vec.transpose(ap(w("ot", 0, 32)), ap(w("on", 0, 32))), [w("on", 0, 32)], [w("ot", 0, 32)])
    dma("y", T.oc[:, 128:1408], ap(w("qx3", 32, 352)).bitcast(dt.uint8), "st", [w("qx3", 32, 352)], [])
    out_scales(32, 352, "sx3", 32, 352)
    for a, z in ((32, 192), (192, 352)):
        dma("y", T.y[:, a:z], ap(w("yo", a, z)), "st", [w("yo", a, z)], [])
    for a, b in ((0, 0), (32, 352)):
        v = w("qh", a, a + 32)
        dma("y", T.oc[:, 4 * b:4 * b + 128], ap(v).bitcast(dt.uint8), "st", [v], [])
        out_scales(b, b + 32, "sh0", a, a + 32)
    for a, b in ((0, 0), (32, 352)):
        v = w("yo2", a, a + 32)
        dma("s", T.y[:, b:b + 32], ap(v), "st", [v], [])
    for m in range(8):
        v = w("ot", 16 * (m % 2), 16 * (m % 2) + 16, 1, 32 * (m // 2), 32 * (m // 2) + 24)
        dma("s", T.op[m:m + 1, :], ap(v), "st", [v], [])
    for sem in SEMAPHORES:
        if total.get(sem, 0):
            wait("g", sem, total[sem])
